import numpy as np, ml_dtypes
CORES = [24,25,26,27,28,29,30,31]
N = 8
BF = ml_dtypes.bfloat16
def f(rng, *shape):
    return (rng.standard_normal(shape, dtype=np.float32) * np.exp2(rng.integers(-2, 3, shape[:-1] + (1,)))).astype(BF)
def wide(rng, *shape):
    v = f(rng, *shape).astype(np.float32); k = shape[:-2] + (1, shape[-1])
    return (v * np.exp2(rng.integers(-6, 7, k)) * (rng.random(k) > 0.0625)).astype(BF)
def gentries(a):
    return np.ascontiguousarray(a.reshape(8, 16, -1).transpose(0, 2, 1)).reshape(8, -1)
def gtable(e):
    e = np.asarray(e); return np.ascontiguousarray(e.reshape(8, -1, 16).transpose(0, 2, 1)).reshape(128, -1).astype(np.int32)
E, D, CAP, S, P = 2048, 2, 256, 4, 4096
def setup_inputs(rng):
    mp = rng.integers(0, 8, (8, S)); mp[:, S - 1] = rng.permutation(8); i, j = rng.permutation(8)[:2]; mp[j, :S - 1] = mp[i, :S - 1]
    sh = (N, 8, D * E); pl = np.where(rng.random(sh) < 0.5, rng.integers(0, E, sh), rng.integers(E, P, sh)); se = rng.integers(0, E, (N, 8, N * CAP))
    return {"x": f(rng, N, 16, E), "mp": np.repeat(mp[None], N, 0).astype(np.int32),
            "src": np.stack([gtable(e) for e in pl]), "snd": np.stack([gtable(e) for e in se]),
            "bs": f(rng, N, 128, 1).astype(np.float32) * np.float32(0.25),
            "aw": rng.standard_normal((N, 16, 16), dtype=np.float32) * np.float32(0.5),
            "ab": rng.standard_normal((N, 16, 1), dtype=np.float32) * np.float32(0.25),
            "aq": np.clip(0.4 * rng.standard_normal((N, 16, 1)), -1, 1).astype(np.float32)}
def setup_inputs_full(rng):
    d = setup_inputs(rng)
    d["src"] = np.stack([gtable(np.stack([E + rng.permutation(D * E) % (N * CAP) for k in range(8)])) for r in range(N)])
    d["snd"] = np.stack([gtable(np.stack([np.concatenate([rng.permutation(E)[:CAP] for q in range(N)]) for k in range(8)])) for r in range(N)]); return d
def setup_inputs_edges(rng):
    d = setup_inputs(rng); ends = np.array([0, E - 1] + [E + q * CAP + i for q in range(N) for i in (0, CAP - 1)])
    pl = rng.choice(ends, (N, 8, D * E)); pl[:, rng.integers(0, 8)] = P - 1; se = rng.choice(np.array([0, E - 1]), (N, 8, N * CAP))
    d["src"] = np.stack([gtable(e) for e in pl]); d["snd"] = np.stack([gtable(e) for e in se]); return d
def setup_inputs_chains(rng):
    d = setup_inputs(rng); c = rng.choice(np.array([0, 7]), (3, S)); c[1, 0] = 0; c[2, 0] = 7; c[:, S - 1] = rng.permutation(8)[:3]; c[0] = c[0, S - 1]
    d["mp"] = np.repeat(c[rng.permutation(np.array([0, 0, 0, 1, 1, 2, 2, 2]))][None], N, 0).astype(np.int32); return d
def setup_inputs_dead(rng):
    d = setup_inputs(rng); k, z = rng.permutation(8)[:2]; d["bs"][:, 16 * k:16 * k + 16] = -4096; d["bs"][:, 16 * z:16 * z + 16] = 0
    g = int(np.flatnonzero(d["mp"][0, :, S - 1] != k)[rng.integers(0, 7)]); d["mp"][:, g, 0] = k; return d
def setup_inputs_spread(rng):
    d = setup_inputs(rng); d["x"] = wide(rng, N, 16, E); return d
def check_inputs(d):
    bad = []
    for a, n in (("src", P), ("snd", E), ("mp", 8)):
        if d[a].min() < 0 or d[a].max() >= n: bad.append("range of " + a)
    if (d["mp"] != d["mp"][:1]).any(): bad.append("mp is the same on all ranks")
    if not (np.abs(d["aq"]) <= 1).all(): bad.append("range of aq")
    for a in ("x", "bs", "aw", "ab", "aq"):
        if not np.isfinite(d[a].astype(np.float32)).all(): bad.append("finite " + a)
    return bad
def reference(x, mp, src, snd, bs, aw, ab, aq):
    h = np.repeat(x.astype(np.float64)[:, None], 8, axis=1)
    pl = np.stack([gentries(a) for a in src]); se = np.stack([gentries(a) for a in snd]).reshape(N, 8, N, CAP); b = bs.astype(np.float64).reshape(N, 8, 16, 1)
    for s in range(S):
        nh = np.zeros_like(h)
        for g in range(8):
            k = int(mp[0, g, s])
            for r in range(N):
                win = np.concatenate([h[r, g]] + [h[q, g][:, se[q, k, r]] for q in range(N)], axis=1)
                v = np.sum(win[:, pl[r, k]].reshape(16, D, E), axis=1)
                nh[r, g] = np.maximum(v * 2.0 ** -1 + b[r, k], 0)
        h = nh
    tot = np.zeros(8, np.float64)
    for r in range(N):
        for g in range(8):
            t = np.tanh(aw[r].astype(np.float64).T @ h[r, g] + ab[r].astype(np.float64))
            tot[g] += np.sum(aq[r].astype(np.float64) * t)
    w = np.exp(tot * 2.0 ** -14)
    y = np.einsum("g,rgce->rce", w, h)
    return {"y": y.astype(np.float32), "w": np.repeat(w[None, :, None], N, axis=0).astype(np.float32)}

@@ -1,0 +1,333 @@
+from concourse.bass import DstId, RemoteDMATransfer
+from concourse.mybir import AluOpType, AxisListType, ActivationFunctionType
+
+E, CAP, S, NR = 2048, 256, 4, 8
+SRC_CHUNKS = [256] * 8
+LAST_CHUNKS = [128, 128, 256, 384, 512, 512, 128]
+NCH = len(LAST_CHUNKS)
+
+SCRATCH = {
+    "mp1": ("sbuf", [128, 32], "int32"),
+    "mpb": ("sbuf", [128, 32], "int32"),
+    "cf": ("sbuf", [128, 128], "float32"),
+    "cs": ("sbuf", [128, 128], "float32"),
+    "offi": ("sbuf", [128, 32], "int32"),
+    "offp": ("sbuf", [128, 32], "uint16"),
+    "sndi": ("sbuf", [128, 128], "int32"),
+    "srci": ("sbuf", [128, 256], "int32"),
+    "tb": ("sbuf", [128, 388], "float32"),
+    "tp": ("sbuf", [128, 256], "float32"),
+    "pm": ("sbuf", [128, 512], "float32"),
+    "bias": ("sbuf", [128, 4], "float32"),
+    "pidx": ("sbuf", [128, 1], "int32"),
+    "bits": ("sbuf", [128, 4], "int32"),
+    "bitf": ("sbuf", [128, 8], "float32"),
+    "colh": ("sbuf", [128, 16], "float32"),
+    "offq": ("sbuf", [128, 16], "uint16"),
+    "mi": ("sbuf", [128, 64], "int32"),
+    "mj": ("sbuf", [128, 64], "int32"),
+    "mask": ("sbuf", [128, 64], "float32"),
+    "bi": ("sbuf", [128, 128], "int32"),
+    "bj": ("sbuf", [128, 128], "int32"),
+    "bm": ("sbuf", [128, 128], "float32"),
+    "rep": ("sbuf", [128, 128], "float32"),
+    "aws": ("sbuf", [128, 16], "float32"),
+    "abq": ("sbuf", [128, 2], "float32"),
+    "awt": ("sbuf", [128, 128], "float32"),
+    "awb": ("sbuf", [128, 128], "float32"),
+    "abc": ("sbuf", [128, 2], "float32"),
+    "hh": ("sbuf", [128, E], "float32"),
+    "th": ("sbuf", [128, E], "float32"),
+    "acc": ("sbuf", [128, 8], "float32"),
+    "vq": ("sbuf", [128, 8], "float32"),
+    "land": ("sbuf", [128, (NR - 1) * NCH], "float32"),
+    "sc": ("sbuf", [128, 4], "float32"),
+    "m1": ("sbuf", [128, 64], "float32"),
+    "wm": ("sbuf", [128, 64], "float32"),
+    "yt": ("sbuf", [128, 256], "float32"),
+}
+for _s in range(S):
+    _d = "bfloat16" if _s == 0 else "float32"
+    SCRATCH["li%d" % _s] = ("sbuf", [128, 384], "uint16")
+    SCRATCH["win%d" % _s] = ("sbuf", [128, 2 * E], _d)
+    SCRATCH["sb%d" % _s] = ("sbuf", [128, (NR - 1) * CAP], _d)
+    SCRATCH["ga%d" % _s] = ("sbuf", [128, E], "float32")
+    SCRATCH["zz%d" % _s] = ("sbuf", [128, E], "float32")
+for _b in range(8):
+    SCRATCH["ps%d" % _b] = ("psum", [128, 512], "float32")
+
+SEMAPHORES = ["cv", "ca", "ct", "cg", "d_mp", "d_snd", "d_x", "d_src", "d_bs", "d_aw", "d_out",
+              "sent", "arr0", "arr1", "arr2", "arr3", "arrs"]
+
+
+def rounds_of(rank, cores, topo):
+    me = cores[rank]
+    same = [r for r in range(len(cores)) if topo.die(cores[r]) == topo.die(me)]
+    other = [r for r in range(len(cores)) if topo.die(cores[r]) != topo.die(me)]
+    i = same.index(rank)
+    near = [same[(i + j) % len(same)] for j in range(1, len(same))]
+    far = [other[(i + j) % len(other)] for j in range(len(other))]
+    out = []
+    for j in range(max(len(near), len(far))):
+        if j < len(near) and j < len(far):
+            out.append([(far[j], topo.engines(me, cores[far[j]])[0::2]),
+                        (near[j], topo.engines(me, cores[near[j]])[1::2])])
+        else:
+            t = far[j] if j < len(far) else near[j]
+            out.append([(t, topo.engines(me, cores[t]))])
+    return out
+
+
+def rank_program(g, core, T, topo):
+    rank = T.rank_of(core)
+    if rank is None:
+        return
+    cores = list(T.cores)
+    A, F, X = AluOpType, ActivationFunctionType, AxisListType.X
+    V, ACT, PE, SY = g.vector, g.scalar, g.tensor, g.sync
+    queues = {"v": V, "a": ACT, "t": PE, "g": g, "s": SY}
+    count = {}
+    seen = {}
+
+    def wait(q, *toks):
+        need = {}
+        for tok in toks:
+            if tok is not None:
+                need[tok[0]] = max(need.get(tok[0], 0), tok[1])
+        for name, val in need.items():
+            if seen.get((q, name), 0) < val:
+                queues[q].wait_ge(T.sem[name], val)
+                seen[(q, name)] = val
+
+    def done(ins, name, n=1):
+        ins.then_inc(T.sem[name], n)
+        count[name] = count.get(name, 0) + n
+        return (name, count[name])
+
+    def v(deps, fn, *a, **k):
+        wait("v", *deps)
+        return done(fn(*a, **k), "cv")
+
+    def act(deps, *a, **k):
+        wait("a", *deps)
+        return done(ACT.activation(*a, **k), "ca")
+
+    def mm(deps, out, lhsT, rhs, start=True, stop=True):
+        wait("t", *deps)
+        return done(PE.matmul(out, lhsT, rhs, start, stop), "ct")
+
+    def gp(deps, fn, *a, **k):
+        wait("g", *deps)
+        return done(fn(*a, **k), "cg")
+
+    def dma(q, deps, sem, out, in_):
+        wait(q, *deps)
+        return done(queues[q].dma_start(out, in_), sem, 16)
+
+    def bitmask(engs):
+        return sum(1 << e for e in engs)
+
+    def dst_id(r):
+        rid, pid, _ = topo.addr(cores[r])
+        return DstId(rid=rid, pnc=pid)
+
+    rounds = rounds_of(rank, cores, topo)
+    arrive = sum(len(engs) for q in range(NR) for call in rounds_of(q, cores, topo) for (t, engs) in call if t == rank)
+    win = [T["win%d" % s] for s in range(S)]
+    li = [T["li%d" % s] for s in range(S)]
+    ps = [T["ps%d" % b] for b in range(8)]
+
+    k_mp = dma("s", [], "d_mp", T.mp1[0:1, :], T.mp[:])
+    k_snd = dma("a", [], "d_snd", T.sndi[:], T.snd[:])
+    for k in range(8):
+        k_x = dma("s" if k % 2 == 0 else "a", [], "d_x", win[0][16 * k:16 * k + 16, 0:E], T.x[:])
+    k_src = dma("s", [], "d_src", T.srci[:], T.src[:])
+    k_bs = dma("a", [], "d_bs", T.tb[:, 384:385], T.bs[:])
+    dma("s", [], "d_aw", T.aws[0:16, :], T.aw[:])
+    dma("s", [], "d_aw", T.abq[0:16, 0:1], T.ab[:])
+    k_aw = dma("s", [], "d_aw", T.abq[0:16, 1:2], T.aq[:])
+
+    k_cf = gp([], g.iota, T.cf[:], [[0, 8], [-1, 16]], 0, 1, allow_small_or_imprecise_dtypes=True)
+    k_oi = gp([], g.iota, T.offi[:], [[1, 4], [4, 8]], 0, 0)
+    k_mpb = gp([k_mp], g.partition_broadcast, T.mpb[:], T.mp1[0:1, :], 128)
+    k_cs = v([k_cf], V.tensor_scalar, T.cs[:], T.cf[:], 1.0 / 16, None, A.mult)
+    k_op = v([k_oi], V.tensor_copy, T.offp[:], T.offi[:])
+    k_sndf = v([k_snd], V.tensor_copy, T.tb[:, 256:384], T.sndi[:])
+
+    def perm(s):
+        return v([k_mpb, k_cs, k_op], V.tensor_tensor, T.pm[:, 128 * s:128 * s + 128],
+                 T.mpb[:, 0:32].indirect(T.offp[:, 8 * s:8 * s + 8]), T.cs[:], A.is_equal)
+
+    def pmat(s):
+        return T.pm[:, 128 * s:128 * s + 128]
+
+    k_p = perm(0)
+    k_m = mm([k_p, k_sndf], ps[0][:, 0:128], pmat(0), T.tb[:, 256:384])
+    k_sl = v([k_m], V.tensor_copy, li[0][:, 256:384], ps[0][:, 0:128])
+
+    def send(s, source, scale, deps):
+        def gather(q, out, t):
+            src_ap = source[:, 0:E].indirect(li[s][:, 256 + 16 * t:256 + 16 * t + 16])
+            if q == "v":
+                if scale is None:
+                    return v(deps, V.tensor_copy, out, src_ap)
+                return v(deps, V.tensor_scalar, out, src_ap, 0.0, scale, A.max, A.mult)
+            if scale is None:
+                return act(deps, out, src_ap, F.Identity)
+            return act(deps, out, src_ap, F.Relu, scale=scale)
+        pos = 0
+        own = None
+        lo = E + CAP * rank
+        for call in rounds:
+            toks, trs = [], []
+            for q, (t, engs) in zip(("v", "a"), call):
+                buf = T["sb%d" % s][:, pos:pos + CAP]
+                pos += CAP
+                toks.append(gather(q, buf, t))
+                trs.append(RemoteDMATransfer(dst_ids=[dst_id(t)], dma_engine_mask=bitmask(engs),
+                                             remote_sem=T.sem["arr%d" % s], src=buf, dst=win[s][:, lo:lo + CAP]))
+                count["sent"] = count.get("sent", 0) + len(engs)
+            if len(call) == 1 and own is None:
+                own = gather("a", win[s][:, lo:lo + CAP], rank)
+            wait("g", *toks)
+            g.remote_dma_fused(trs, local_sem=T.sem.sent)
+        if own is None:
+            own = gather("a", win[s][:, lo:lo + CAP], rank)
+        return own
+
+    def own_part(s, z, scale, deps):
+        h = E // 2
+        a = v(deps, V.tensor_scalar, win[s][:, 0:h], z[:, 0:h], 0.0, scale, A.max, A.mult)
+        b = act(deps, win[s][:, h:E], z[:, h:E], F.Relu, scale=scale)
+        return [a, b]
+
+    def source(s, d, lo, n):
+        c = 128 * d + lo // 16
+        return win[s][:, :].indirect(li[s][:, c:c + n // 16])
+
+    def step(s, deps):
+        ga, zz = T["ga%d" % s], T["zz%d" % s]
+        lo = 0
+        for n in SRC_CHUNKS:
+            a = act(deps, ga[:, lo:lo + n], source(s, 0, lo, n), F.Identity, bias=T.bias[:, s:s + 1])
+            z = v(deps + [a], V.tensor_tensor, zz[:, lo:lo + n], source(s, 1, lo, n), ga[:, lo:lo + n], A.add)
+            lo += n
+        return z
+
+    def lists(s, k_mat):
+        v([k_mat], V.tensor_copy, li[s][:, 0:384], ps[s + 1][:, 0:384])
+        return v([k_mat], V.tensor_copy, T.bias[:, s:s + 1], ps[s + 1][:, 384:385])
+
+    k_own = send(0, win[0], None, [k_sl, k_x])
+    k_srcf = v([k_src], V.tensor_copy, T.tb[:, 0:256], T.srci[:])
+    mm([k_srcf], ps[1][:, 0:256], pmat(0), T.tb[:, 0:256])
+    k_m0 = mm([k_bs], ps[1][:, 256:257], pmat(0), T.tb[:, 384:385])
+    k_m1 = mm([perm(1)], ps[2][:, 0:385], pmat(1), T.tb[:, 0:385])
+    k_m2 = mm([perm(2)], ps[3][:, 0:385], pmat(2), T.tb[:, 0:385])
+    k_p3 = perm(3)
+    v([k_m0], V.tensor_copy, li[0][:, 0:256], ps[1][:, 0:256])
+    k_l0 = v([k_m0], V.tensor_scalar, T.bias[:, 0:1], ps[1][:, 256:257], 2.0, None, A.mult)
+    k_l1 = lists(1, k_m1)
+    k_pi = gp([], g.iota, T.pidx[:], [[0, 1]], 0, 1)
+    k_ch = gp([], g.iota, T.colh[:], [[64, 2], [1, 8]], 0, 0, allow_small_or_imprecise_dtypes=True)
+    k_mi = gp([], g.iota, T.mi[:], [[1, 2], [-1, 32]], 32, 2)
+    k_bi = gp([], g.iota, T.bi[:], [[-16, 8], [0, 16]], 0, 1)
+    k_z = step(0, [("arr0", arrive), k_own, k_l0, k_x])
+
+    k_own = send(1, T.zz0, 0.25, [k_z, k_l1])
+    k_h = own_part(1, T.zz0, 0.25, [k_z])
+    k_l2 = lists(2, k_m2)
+    v([k_pi], V.tensor_scalar, T.bits[:, 0:1], T.pidx[:], 7, None, A.bitwise_and)
+    v([k_pi], V.tensor_scalar, T.bits[:, 1:2], T.pidx[:], 8, None, A.bitwise_and)
+    k = v([k_pi], V.tensor_scalar, T.bits[:, 2:3], T.pidx[:], 1, None, A.bitwise_and)
+    k = v([k], V.tensor_copy, T.bitf[:, 0:3], T.bits[:, 0:3])
+    k = v([k], V.tensor_scalar, T.bitf[:, 3:4], T.bitf[:, 0:1], 8.0, T.bitf[:, 1:2], A.mult, A.add)
+    k = v([k], V.tensor_scalar, T.bitf[:, 4:5], T.bitf[:, 2:3], -7.5, T.bitf[:, 3:4], A.mult, A.add)
+    k = v([k, k_ch], V.tensor_scalar, T.offq[:], T.colh[:], T.bitf[:, 4:5], 2.0, A.add, A.mult)
+    k = v([k, k_srcf], V.tensor_copy, T.tp[:], T.tb[:, 0:256].indirect(T.offq[:, 0:16]))
+    mm([k, k_p3], ps[4][:, 0:256], pmat(3), T.tp[:])
+    k_m3 = mm([], ps[4][:, 256:385], pmat(3), T.tb[:, 256:385])
+    k_z = step(1, [("arr1", arrive), k_own, k_l1] + k_h)
+
+    k_own = send(2, T.zz1, 0.5, [k_z, k_l2])
+    k_h = own_part(2, T.zz1, 0.5, [k_z])
+    k_l3 = lists(3, k_m3)
+    k_rep = v([k_cf], V.tensor_scalar, T.rep[0:16, :], T.cf[0:16, :], 0.0, None, A.is_equal)
+    k_t1 = mm([k_rep, k_aw], ps[5][0:16, 0:128], T.aws[0:16, :], T.rep[0:16, :])
+    k_t3 = mm([], ps[7][:, 80:82], T.rep[0:16, :], T.abq[0:16, :])
+    k = v([k_bi], V.tensor_scalar, T.bj[:], T.bi[:], 4, None, A.arith_shift_right)
+    k_bm = v([k], V.tensor_scalar, T.bm[:], T.bj[:], 0.0, None, A.is_equal)
+    k = v([k_t1], V.tensor_copy, T.awt[0:16, :], ps[5][0:16, 0:128])
+    k_t2 = mm([k], ps[6][:, 0:128], T.awt[0:16, :], T.rep[0:16, :])
+    k_z = step(2, [("arr2", arrive), k_own, k_l2] + k_h)
+
+    k_own = send(3, T.zz2, 0.5, [k_z, k_l3])
+    k_h = own_part(3, T.zz2, 0.5, [k_z])
+    k_abc = v([k_t3], V.tensor_copy, T.abc[:], ps[7][:, 80:82])
+    k_awb = v([k_t2, k_bm], V.tensor_tensor, T.awb[:], T.bm[:], ps[6][:, 0:128], A.mult)
+    k = v([k_mi], V.tensor_scalar, T.mj[:], T.mi[:], 31, None, A.bitwise_and)
+    k_mask = v([k], V.tensor_scalar, T.mask[:], T.mj[:], 0.0, None, A.is_equal)
+    deps = [("arr3", arrive), k_own, k_l3] + k_h
+    starts = [sum(LAST_CHUNKS[:j]) for j in range(NCH)]
+    gat = {}
+    for j in range(NCH):
+        lo, n = starts[j], LAST_CHUNKS[j]
+        if j < 2:
+            gat[j] = v(deps, V.tensor_scalar, T.ga3[:, lo:lo + n], source(3, 0, lo, n), T.bias[:, 3:4], None, A.add)
+        else:
+            gat[j] = act(deps, T.ga3[:, lo:lo + n], source(3, 0, lo, n), F.Identity, bias=T.bias[:, 3:4])
+
+    def zsum(j):
+        lo, n = starts[j], LAST_CHUNKS[j]
+        return v([gat[j]], V.tensor_tensor, T.zz3[:, lo:lo + n], source(3, 1, lo, n), T.ga3[:, lo:lo + n], A.add)
+
+    kz = zsum(0)
+    pre = []
+    for j in range(NCH):
+        lo, n = starts[j], LAST_CHUNKS[j]
+        nxt = zsum(j + 1) if j in (0, NCH - 2) else None
+        kh = v([kz], V.tensor_scalar, T.hh[:, lo:lo + n], T.zz3[:, lo:lo + n], 0.0, None, A.max)
+        pre.append(mm([kh, k_awb], ps[j][:, 0:n], T.awb[:], T.hh[:, lo:lo + n]))
+        if nxt is None and j + 1 < NCH:
+            nxt = zsum(j + 1)
+        kz = nxt
+    for j in range(NCH):
+        lo, n = starts[j], LAST_CHUNKS[j]
+        k_t = act([pre[j], k_abc], T.th[:, lo:lo + n], ps[j][:, 0:n], F.Tanh, bias=T.abc[:, 0:1],
+                  accum_out=T.acc[:, j:j + 1])
+    k_vq = v([k_t], V.tensor_scalar, T.vq[:, 0:NCH], T.acc[:, 0:NCH], T.abc[:, 1:2], None, A.mult)
+
+    others = [t for t in range(NR) if t != rank]
+    engs = topo.engines(core, cores[others[0]])
+    dsts = []
+    for t in others:
+        j = [q for q in range(NR) if q != t].index(rank)
+        dsts.append(T.land[:, NCH * j:NCH * j + NCH])
+    wait("g", k_vq)
+    g.remote_dma_fused([RemoteDMATransfer(dst_ids=[dst_id(t) for t in others], dma_engine_mask=bitmask(engs),
+                                          remote_sem=T.sem.arrs, srcs=[T.vq[:, 0:NCH]], dsts=dsts)],
+                       local_sem=T.sem.sent)
+    count["sent"] += len(engs)
+    inv = 1.0 / (NR * E)
+    k = mm([k_vq, k_bm], ps[7][:, 0:NCH], T.bm[:], T.vq[:, 0:NCH])
+    k_so = v([k], V.tensor_reduce, T.sc[:, 0:1], ps[7][:, 0:NCH], X, A.add)
+    k = act([k_so], T.sc[:, 1:2], T.sc[:, 0:1], F.Exp, scale=inv)
+    k_m1 = v([k, k_mask], V.tensor_scalar, T.m1[:], T.mask[:], T.sc[:, 1:2], None, A.mult)
+    nl = (NR - 1) * NCH
+    k = mm([("arrs", (NR - 1) * len(engs)), k_so], ps[7][:, 16:16 + nl], T.bm[:], T.land[:])
+    k = v([k], V.tensor_reduce, T.sc[:, 2:3], ps[7][:, 16:16 + nl], X, A.add)
+    k = act([k], T.sc[:, 3:4], T.sc[:, 2:3], F.Exp, scale=inv)
+    k_wm = v([k, k_m1], V.tensor_scalar, T.wm[:], T.m1[:], T.sc[:, 3:4], None, A.mult)
+    dma("s", [k_wm], "d_out", T.w[:], T.wm[0:128:16, 0:1])
+
+    for bank, bs_ in enumerate([(0, 1, 2, 3), (4, 5, 6), (7,)]):
+        for i, b in enumerate(bs_):
+            for par in range(2):
+                c = 128 * (2 * b + par)
+                k = mm([k_wm], ps[bank][:, 32 * i:32 * i + 32], T.hh[:, c:c + 128], T.wm[:, 32 * par:32 * par + 32],
+                       par == 0, par == 1)
+        k_y = v([k], V.transpose, T.yt[:, 32 * bs_[0]:32 * bs_[-1] + 32], ps[bank][:, 0:32 * len(bs_)])
+    for a in range(4):
+        k_o = dma("s" if a % 2 == 0 else "a", [k_y], "d_out", T.y[:, 512 * a:512 * a + 512], T.yt[32 * a:32 * a + 32, :])
+    wait("s", k_o)
+    wait("g", *[(n, count[n]) for n in ("sent", "cg", "ct", "ca", "cv")])

@@ -2,8 +2,9 @@ from concourse.bass import DstId, RemoteDMATransfer
 from concourse.mybir import AluOpType, AxisListType, ActivationFunctionType
 
 E, CAP, S, NR = 2048, 256, 4, 8
-SRC_CHUNKS = [256] * 8
-LAST_CHUNKS = [128, 128, 256, 384, 512, 512, 128]
+SRC_CHUNKS = [160, 320, 320, 320, 320, 320, 288]
+RELU_V = 704
+LAST_CHUNKS = [160, 256, 384, 480, 384, 256, 128]
 NCH = len(LAST_CHUNKS)
 
 SCRATCH = {
@@ -30,19 +31,23 @@ SCRATCH = {
     "bi": ("sbuf", [128, 128], "int32"),
     "bj": ("sbuf", [128, 128], "int32"),
     "bm": ("sbuf", [128, 128], "float32"),
+    "bmq": ("sbuf", [128, 128], "float32"),
     "rep": ("sbuf", [128, 128], "float32"),
     "aws": ("sbuf", [128, 16], "float32"),
-    "abq": ("sbuf", [128, 2], "float32"),
+    "abs_": ("sbuf", [128, 1], "float32"),
+    "aqs": ("sbuf", [128, 1], "float32"),
+    "aql": ("sbuf", [128, NR - 1], "float32"),
+    "aqx": ("sbuf", [128, (NR - 1) * NCH], "float32"),
     "awt": ("sbuf", [128, 128], "float32"),
     "awb": ("sbuf", [128, 128], "float32"),
     "abc": ("sbuf", [128, 2], "float32"),
     "hh": ("sbuf", [128, E], "float32"),
     "th": ("sbuf", [128, E], "float32"),
     "acc": ("sbuf", [128, 8], "float32"),
-    "vq": ("sbuf", [128, 8], "float32"),
+    "eo": ("sbuf", [128, 8], "float32"),
     "land": ("sbuf", [128, (NR - 1) * NCH], "float32"),
+    "lq": ("sbuf", [128, (NR - 1) * NCH], "float32"),
     "sc": ("sbuf", [128, 4], "float32"),
-    "m1": ("sbuf", [128, 64], "float32"),
     "wm": ("sbuf", [128, 64], "float32"),
     "yt": ("sbuf", [128, 256], "float32"),
 }
@@ -56,8 +61,8 @@ for _s in range(S):
 for _b in range(8):
     SCRATCH["ps%d" % _b] = ("psum", [128, 512], "float32")
 
-SEMAPHORES = ["cv", "ca", "ct", "cg", "d_mp", "d_snd", "d_x", "d_src", "d_bs", "d_aw", "d_out",
-              "sent", "arr0", "arr1", "arr2", "arr3", "arrs"]
+SEMAPHORES = ["cv", "ca", "ct", "cg", "d_mp", "d_snd", "d_x", "d_src", "d_bs", "d_aw", "d_aq", "d_out",
+              "sent", "arr0", "arr1", "arr2", "arr3", "arrq", "arrs"]
 
 
 def rounds_of(rank, cores, topo):
@@ -86,7 +91,7 @@ def rank_program(g, core, T, topo):
     A, F, X = AluOpType, ActivationFunctionType, AxisListType.X
     V, ACT, PE, SY = g.vector, g.scalar, g.tensor, g.sync
     queues = {"v": V, "a": ACT, "t": PE, "g": g, "s": SY}
-    count = {}
+    count = {"sent": 0}
     seen = {}
 
     def wait(q, *toks):
@@ -131,27 +136,53 @@ def rank_program(g, core, T, topo):
         rid, pid, _ = topo.addr(cores[r])
         return DstId(rid=rid, pnc=pid)
 
+    others = [t for t in range(NR) if t != rank]
+    all_engs = topo.engines(core, cores[others[0]])
+
+    def to_all(deps, src, buf, n, sem):
+        dsts = []
+        for t in others:
+            j = [q for q in range(NR) if q != t].index(rank)
+            dsts.append(buf[:, n * j:n * j + n])
+        wait("g", *deps)
+        g.remote_dma_fused([RemoteDMATransfer(dst_ids=[dst_id(t) for t in others], dma_engine_mask=bitmask(all_engs),
+                                              remote_sem=T.sem[sem], srcs=[src], dsts=dsts)], local_sem=T.sem.sent)
+        count["sent"] += len(all_engs)
+        return (sem, (NR - 1) * len(all_engs))
+
     rounds = rounds_of(rank, cores, topo)
     arrive = sum(len(engs) for q in range(NR) for call in rounds_of(q, cores, topo) for (t, engs) in call if t == rank)
     win = [T["win%d" % s] for s in range(S)]
     li = [T["li%d" % s] for s in range(S)]
     ps = [T["ps%d" % b] for b in range(8)]
 
+    k_zero = v([], V.memset, T.aqs[:], 0.0)
     k_mp = dma("s", [], "d_mp", T.mp1[0:1, :], T.mp[:])
     k_snd = dma("a", [], "d_snd", T.sndi[:], T.snd[:])
     for k in range(8):
         k_x = dma("s" if k % 2 == 0 else "a", [], "d_x", win[0][16 * k:16 * k + 16, 0:E], T.x[:])
+        if k == 0:
+            k_aq = dma("s", [k_zero], "d_aq", T.aqs[0:16, :], T.aq[:])
     k_src = dma("s", [], "d_src", T.srci[:], T.src[:])
     k_bs = dma("a", [], "d_bs", T.tb[:, 384:385], T.bs[:])
     dma("s", [], "d_aw", T.aws[0:16, :], T.aw[:])
-    dma("s", [], "d_aw", T.abq[0:16, 0:1], T.ab[:])
-    k_aw = dma("s", [], "d_aw", T.abq[0:16, 1:2], T.aq[:])
+    k_aw = dma("s", [], "d_aw", T.abs_[0:16, :], T.ab[:])
 
     k_cf = gp([], g.iota, T.cf[:], [[0, 8], [-1, 16]], 0, 1, allow_small_or_imprecise_dtypes=True)
     k_oi = gp([], g.iota, T.offi[:], [[1, 4], [4, 8]], 0, 0)
+    k_pi = gp([], g.iota, T.pidx[:], [[0, 1]], 0, 1)
+    k_ch = gp([], g.iota, T.colh[:], [[64, 2], [1, 8]], 0, 0, allow_small_or_imprecise_dtypes=True)
     k_mpb = gp([k_mp], g.partition_broadcast, T.mpb[:], T.mp1[0:1, :], 128)
+    k_aql = to_all([k_aq], T.aqs[:], T.aql, 1, "arrq")
     k_cs = v([k_cf], V.tensor_scalar, T.cs[:], T.cf[:], 1.0 / 16, None, A.mult)
     k_op = v([k_oi], V.tensor_copy, T.offp[:], T.offi[:])
+    v([k_pi], V.tensor_scalar, T.bits[:, 0:1], T.pidx[:], 7, None, A.bitwise_and)
+    v([k_pi], V.tensor_scalar, T.bits[:, 1:2], T.pidx[:], 8, None, A.bitwise_and)
+    k = v([k_pi], V.tensor_scalar, T.bits[:, 2:3], T.pidx[:], 1, None, A.bitwise_and)
+    k = v([k], V.tensor_copy, T.bitf[:, 0:3], T.bits[:, 0:3])
+    k = v([k], V.tensor_scalar, T.bitf[:, 3:4], T.bitf[:, 0:1], 8.0, T.bitf[:, 1:2], A.mult, A.add)
+    k = v([k], V.tensor_scalar, T.bitf[:, 4:5], T.bitf[:, 2:3], -7.5, T.bitf[:, 3:4], A.mult, A.add)
+    k_oq = v([k, k_ch], V.tensor_scalar, T.offq[:], T.colh[:], T.bitf[:, 4:5], 2.0, A.add, A.mult)
     k_sndf = v([k_snd], V.tensor_copy, T.tb[:, 256:384], T.sndi[:])
 
     def perm(s):
@@ -163,11 +194,14 @@ def rank_program(g, core, T, topo):
 
     k_p = perm(0)
     k_m = mm([k_p, k_sndf], ps[0][:, 0:128], pmat(0), T.tb[:, 256:384])
+    k_p1 = perm(1)
     k_sl = v([k_m], V.tensor_copy, li[0][:, 256:384], ps[0][:, 0:128])
+    k_ms1 = mm([k_p1], ps[2][:, 0:128], pmat(1), T.tb[:, 256:384])
 
     def send(s, source, scale, deps):
-        def gather(q, out, t):
-            src_ap = source[:, 0:E].indirect(li[s][:, 256 + 16 * t:256 + 16 * t + 16])
+        def gather(q, out, t, a=0, n=CAP):
+            c = 256 + 16 * t + a // 16
+            src_ap = source[:, 0:E].indirect(li[s][:, c:c + n // 16])
             if q == "v":
                 if scale is None:
                     return v(deps, V.tensor_copy, out, src_ap)
@@ -176,27 +210,26 @@ def rank_program(g, core, T, topo):
                 return act(deps, out, src_ap, F.Identity)
             return act(deps, out, src_ap, F.Relu, scale=scale)
         pos = 0
-        own = None
         lo = E + CAP * rank
+        sb = T["sb%d" % s]
         for call in rounds:
             toks, trs = [], []
             for q, (t, engs) in zip(("v", "a"), call):
-                buf = T["sb%d" % s][:, pos:pos + CAP]
+                if len(call) == 1:
+                    h = CAP // 2
+                    toks += [gather("v", sb[:, pos:pos + h], t, 0, h), gather("a", sb[:, pos + h:pos + CAP], t, h, h)]
+                else:
+                    toks.append(gather(q, sb[:, pos:pos + CAP], t))
+                trs.append(RemoteDMATransfer(dst_ids=[dst_id(t)], dma_engine_mask=bitmask(engs), remote_sem=T.sem["arr%d" % s],
+                                             src=sb[:, pos:pos + CAP], dst=win[s][:, lo:lo + CAP]))
                 pos += CAP
-                toks.append(gather(q, buf, t))
-                trs.append(RemoteDMATransfer(dst_ids=[dst_id(t)], dma_engine_mask=bitmask(engs),
-                                             remote_sem=T.sem["arr%d" % s], src=buf, dst=win[s][:, lo:lo + CAP]))
-                count["sent"] = count.get("sent", 0) + len(engs)
-            if len(call) == 1 and own is None:
-                own = gather("a", win[s][:, lo:lo + CAP], rank)
+                count["sent"] += len(engs)
             wait("g", *toks)
             g.remote_dma_fused(trs, local_sem=T.sem.sent)
-        if own is None:
-            own = gather("a", win[s][:, lo:lo + CAP], rank)
-        return own
+        return gather("a", win[s][:, lo:lo + CAP], rank)
 
     def own_part(s, z, scale, deps):
-        h = E // 2
+        h = RELU_V
         a = v(deps, V.tensor_scalar, win[s][:, 0:h], z[:, 0:h], 0.0, scale, A.max, A.mult)
         b = act(deps, win[s][:, h:E], z[:, h:E], F.Relu, scale=scale)
         return [a, b]
@@ -205,12 +238,20 @@ def rank_program(g, core, T, topo):
         c = 128 * d + lo // 16
         return win[s][:, :].indirect(li[s][:, c:c + n // 16])
 
-    def step(s, deps):
+    def first_source(q, s, lo, n, deps):
+        ga = T["ga%d" % s]
+        if q == "v":
+            return v(deps, V.tensor_scalar, ga[:, lo:lo + n], source(s, 0, lo, n), T.bias[:, s:s + 1], None, A.add)
+        return act(deps, ga[:, lo:lo + n], source(s, 0, lo, n), F.Identity, bias=T.bias[:, s:s + 1])
+
+    def second_source(s, lo, n, deps):
         ga, zz = T["ga%d" % s], T["zz%d" % s]
+        return v(deps, V.tensor_tensor, zz[:, lo:lo + n], source(s, 1, lo, n), ga[:, lo:lo + n], A.add)
+
+    def step(s, deps):
         lo = 0
-        for n in SRC_CHUNKS:
-            a = act(deps, ga[:, lo:lo + n], source(s, 0, lo, n), F.Identity, bias=T.bias[:, s:s + 1])
-            z = v(deps + [a], V.tensor_tensor, zz[:, lo:lo + n], source(s, 1, lo, n), ga[:, lo:lo + n], A.add)
+        for j, n in enumerate(SRC_CHUNKS):
+            z = second_source(s, lo, n, [first_source("v" if j == 0 else "a", s, lo, n, deps)])
             lo += n
         return z
 
@@ -220,104 +261,78 @@ def rank_program(g, core, T, topo):
 
     k_own = send(0, win[0], None, [k_sl, k_x])
     k_srcf = v([k_src], V.tensor_copy, T.tb[:, 0:256], T.srci[:])
-    mm([k_srcf], ps[1][:, 0:256], pmat(0), T.tb[:, 0:256])
-    k_m0 = mm([k_bs], ps[1][:, 256:257], pmat(0), T.tb[:, 384:385])
-    k_m1 = mm([perm(1)], ps[2][:, 0:385], pmat(1), T.tb[:, 0:385])
+    mm([k_bs], ps[1][:, 256:257], pmat(0), T.tb[:, 384:385])
+    k_m0 = mm([k_srcf], ps[1][:, 0:256], pmat(0), T.tb[:, 0:256])
+    mm([], ps[5][:, 256:257], pmat(1), T.tb[:, 384:385])
+    k_m1 = mm([], ps[5][:, 0:256], pmat(1), T.tb[:, 0:256])
+    k_s1 = v([k_ms1], V.tensor_copy, li[1][:, 256:384], ps[2][:, 0:128])
     k_m2 = mm([perm(2)], ps[3][:, 0:385], pmat(2), T.tb[:, 0:385])
-    k_p3 = perm(3)
     v([k_m0], V.tensor_copy, li[0][:, 0:256], ps[1][:, 0:256])
     k_l0 = v([k_m0], V.tensor_scalar, T.bias[:, 0:1], ps[1][:, 256:257], 2.0, None, A.mult)
-    k_l1 = lists(1, k_m1)
-    k_pi = gp([], g.iota, T.pidx[:], [[0, 1]], 0, 1)
-    k_ch = gp([], g.iota, T.colh[:], [[64, 2], [1, 8]], 0, 0, allow_small_or_imprecise_dtypes=True)
     k_mi = gp([], g.iota, T.mi[:], [[1, 2], [-1, 32]], 32, 2)
     k_bi = gp([], g.iota, T.bi[:], [[-16, 8], [0, 16]], 0, 1)
     k_z = step(0, [("arr0", arrive), k_own, k_l0, k_x])
 
-    k_own = send(1, T.zz0, 0.25, [k_z, k_l1])
+    k_own = send(1, T.zz0, 0.25, [k_z, k_s1])
     k_h = own_part(1, T.zz0, 0.25, [k_z])
+    v([k_m1], V.tensor_copy, li[1][:, 0:256], ps[5][:, 0:256])
+    k_l1 = v([k_m1], V.tensor_copy, T.bias[:, 1:2], ps[5][:, 256:257])
     k_l2 = lists(2, k_m2)
-    v([k_pi], V.tensor_scalar, T.bits[:, 0:1], T.pidx[:], 7, None, A.bitwise_and)
-    v([k_pi], V.tensor_scalar, T.bits[:, 1:2], T.pidx[:], 8, None, A.bitwise_and)
-    k = v([k_pi], V.tensor_scalar, T.bits[:, 2:3], T.pidx[:], 1, None, A.bitwise_and)
-    k = v([k], V.tensor_copy, T.bitf[:, 0:3], T.bits[:, 0:3])
-    k = v([k], V.tensor_scalar, T.bitf[:, 3:4], T.bitf[:, 0:1], 8.0, T.bitf[:, 1:2], A.mult, A.add)
-    k = v([k], V.tensor_scalar, T.bitf[:, 4:5], T.bitf[:, 2:3], -7.5, T.bitf[:, 3:4], A.mult, A.add)
-    k = v([k, k_ch], V.tensor_scalar, T.offq[:], T.colh[:], T.bitf[:, 4:5], 2.0, A.add, A.mult)
-    k = v([k, k_srcf], V.tensor_copy, T.tp[:], T.tb[:, 0:256].indirect(T.offq[:, 0:16]))
-    mm([k, k_p3], ps[4][:, 0:256], pmat(3), T.tp[:])
-    k_m3 = mm([], ps[4][:, 256:385], pmat(3), T.tb[:, 256:385])
+    k_rep = v([k_cf], V.tensor_scalar, T.rep[0:16, :], T.cf[0:16, :], 0.0, None, A.is_equal)
+    k_t1 = mm([k_rep, k_aw], ps[5][0:16, 0:128], T.aws[0:16, :], T.rep[0:16, :])
+    mm([], ps[7][:, 80:81], T.rep[0:16, :], T.abs_[0:16, :])
+    mm([k_aq], ps[7][:, 81:82], T.rep[0:16, :], T.aqs[0:16, :])
+    k_t3 = mm([k_aql], ps[7][:, 88:88 + NR - 1], T.rep[0:16, :], T.aql[0:16, :])
     k_z = step(1, [("arr1", arrive), k_own, k_l1] + k_h)
 
     k_own = send(2, T.zz1, 0.5, [k_z, k_l2])
+    k_p3 = perm(3)
+    mm([k_p3], ps[4][:, 256:385], pmat(3), T.tb[:, 256:385])
+    k = v([k_oq, k_srcf], V.tensor_copy, T.tp[:], T.tb[:, 0:256].indirect(T.offq[:, 0:16]))
+    k_m3 = mm([k], ps[4][:, 0:256], pmat(3), T.tp[:])
     k_h = own_part(2, T.zz1, 0.5, [k_z])
     k_l3 = lists(3, k_m3)
-    k_rep = v([k_cf], V.tensor_scalar, T.rep[0:16, :], T.cf[0:16, :], 0.0, None, A.is_equal)
-    k_t1 = mm([k_rep, k_aw], ps[5][0:16, 0:128], T.aws[0:16, :], T.rep[0:16, :])
-    k_t3 = mm([], ps[7][:, 80:82], T.rep[0:16, :], T.abq[0:16, :])
-    k = v([k_bi], V.tensor_scalar, T.bj[:], T.bi[:], 4, None, A.arith_shift_right)
-    k_bm = v([k], V.tensor_scalar, T.bm[:], T.bj[:], 0.0, None, A.is_equal)
-    k = v([k_t1], V.tensor_copy, T.awt[0:16, :], ps[5][0:16, 0:128])
-    k_t2 = mm([k], ps[6][:, 0:128], T.awt[0:16, :], T.rep[0:16, :])
     k_z = step(2, [("arr2", arrive), k_own, k_l2] + k_h)
 
     k_own = send(3, T.zz2, 0.5, [k_z, k_l3])
+    k = v([k_t1], V.tensor_copy, T.awt[0:16, :], ps[5][0:16, 0:128])
+    k_t2 = mm([k], ps[6][:, 0:128], T.awt[0:16, :], T.rep[0:16, :])
+    k = v([k_bi], V.tensor_scalar, T.bj[:], T.bi[:], 4, None, A.arith_shift_right)
     k_h = own_part(3, T.zz2, 0.5, [k_z])
+    k_bm = v([k], V.tensor_scalar, T.bm[:], T.bj[:], 0.0, None, A.is_equal)
     k_abc = v([k_t3], V.tensor_copy, T.abc[:], ps[7][:, 80:82])
     k_awb = v([k_t2, k_bm], V.tensor_tensor, T.awb[:], T.bm[:], ps[6][:, 0:128], A.mult)
-    k = v([k_mi], V.tensor_scalar, T.mj[:], T.mi[:], 31, None, A.bitwise_and)
-    k_mask = v([k], V.tensor_scalar, T.mask[:], T.mj[:], 0.0, None, A.is_equal)
+    k_bmq = v([k_abc], V.tensor_scalar, T.bmq[:], T.bm[:], T.abc[:, 1:2], None, A.mult)
     deps = [("arr3", arrive), k_own, k_l3] + k_h
     starts = [sum(LAST_CHUNKS[:j]) for j in range(NCH)]
-    gat = {}
-    for j in range(NCH):
-        lo, n = starts[j], LAST_CHUNKS[j]
-        if j < 2:
-            gat[j] = v(deps, V.tensor_scalar, T.ga3[:, lo:lo + n], source(3, 0, lo, n), T.bias[:, 3:4], None, A.add)
-        else:
-            gat[j] = act(deps, T.ga3[:, lo:lo + n], source(3, 0, lo, n), F.Identity, bias=T.bias[:, 3:4])
-
-    def zsum(j):
-        lo, n = starts[j], LAST_CHUNKS[j]
-        return v([gat[j]], V.tensor_tensor, T.zz3[:, lo:lo + n], source(3, 1, lo, n), T.ga3[:, lo:lo + n], A.add)
-
-    kz = zsum(0)
+    gat = [first_source("v" if j == 0 else "a", 3, starts[j], LAST_CHUNKS[j], deps) for j in range(NCH)]
     pre = []
     for j in range(NCH):
         lo, n = starts[j], LAST_CHUNKS[j]
-        nxt = zsum(j + 1) if j in (0, NCH - 2) else None
+        kz = second_source(3, lo, n, [gat[j]])
         kh = v([kz], V.tensor_scalar, T.hh[:, lo:lo + n], T.zz3[:, lo:lo + n], 0.0, None, A.max)
         pre.append(mm([kh, k_awb], ps[j][:, 0:n], T.awb[:], T.hh[:, lo:lo + n]))
-        if nxt is None and j + 1 < NCH:
-            nxt = zsum(j + 1)
-        kz = nxt
     for j in range(NCH):
         lo, n = starts[j], LAST_CHUNKS[j]
         k_t = act([pre[j], k_abc], T.th[:, lo:lo + n], ps[j][:, 0:n], F.Tanh, bias=T.abc[:, 0:1],
                   accum_out=T.acc[:, j:j + 1])
-    k_vq = v([k_t], V.tensor_scalar, T.vq[:, 0:NCH], T.acc[:, 0:NCH], T.abc[:, 1:2], None, A.mult)
 
-    others = [t for t in range(NR) if t != rank]
-    engs = topo.engines(core, cores[others[0]])
-    dsts = []
-    for t in others:
-        j = [q for q in range(NR) if q != t].index(rank)
-        dsts.append(T.land[:, NCH * j:NCH * j + NCH])
-    wait("g", k_vq)
-    g.remote_dma_fused([RemoteDMATransfer(dst_ids=[dst_id(t) for t in others], dma_engine_mask=bitmask(engs),
-                                          remote_sem=T.sem.arrs, srcs=[T.vq[:, 0:NCH]], dsts=dsts)],
-                       local_sem=T.sem.sent)
-    count["sent"] += len(engs)
+    k_land = to_all([k_t], T.acc[:, 0:NCH], T.land, NCH, "arrs")
     inv = 1.0 / (NR * E)
-    k = mm([k_vq, k_bm], ps[7][:, 0:NCH], T.bm[:], T.vq[:, 0:NCH])
-    k_so = v([k], V.tensor_reduce, T.sc[:, 0:1], ps[7][:, 0:NCH], X, A.add)
-    k = act([k_so], T.sc[:, 1:2], T.sc[:, 0:1], F.Exp, scale=inv)
-    k_m1 = v([k, k_mask], V.tensor_scalar, T.m1[:], T.mask[:], T.sc[:, 1:2], None, A.mult)
     nl = (NR - 1) * NCH
-    k = mm([("arrs", (NR - 1) * len(engs)), k_so], ps[7][:, 16:16 + nl], T.bm[:], T.land[:])
-    k = v([k], V.tensor_reduce, T.sc[:, 2:3], ps[7][:, 16:16 + nl], X, A.add)
-    k = act([k], T.sc[:, 3:4], T.sc[:, 2:3], F.Exp, scale=inv)
-    k_wm = v([k, k_m1], V.tensor_scalar, T.wm[:], T.m1[:], T.sc[:, 3:4], None, A.mult)
+    for j in range(NR - 1):
+        k_aqx = v([k_t3], V.tensor_scalar, T.aqx[:, NCH * j:NCH * j + NCH], T.cf[:, 0:NCH], 0.0,
+                  ps[7][:, 88 + j:89 + j], A.mult, A.add)
+    k = v([k_mi], V.tensor_scalar, T.mj[:], T.mi[:], 31, None, A.bitwise_and)
+    k_mask = v([k], V.tensor_scalar, T.mask[:], T.mj[:], 0.0, None, A.is_equal)
+    k = mm([k_t, k_bmq], ps[3][:, 0:NCH], T.bmq[:], T.acc[:, 0:NCH])
+    k_eo = act([k], T.eo[:, 0:NCH], ps[3][:, 0:NCH], F.Exp, scale=inv)
+    k = v([k_land, k_aqx], V.tensor_tensor, T.lq[:], T.land[:], T.aqx[:], A.mult)
+    k = mm([k], ps[4][:, 0:nl], T.bm[:], T.lq[:])
+    k = v([k], V.tensor_reduce, T.sc[:, 2:3], ps[4][:, 0:nl], X, A.add)
+    k_er = act([k], T.sc[:, 3:4], T.sc[:, 2:3], F.Exp, scale=inv)
+    k_eo = v([k_eo], V.tensor_reduce, T.sc[:, 1:2], T.eo[:, 0:NCH], X, A.mult)
+    k_wm = v([k_er, k_eo, k_mask], V.tensor_scalar, T.wm[:], T.mask[:], T.sc[:, 1:2], T.sc[:, 3:4], A.mult, A.mult)
     dma("s", [k_wm], "d_out", T.w[:], T.wm[0:128:16, 0:1])
 
     for bank, bs_ in enumerate([(0, 1, 2, 3), (4, 5, 6), (7,)]):

@@ -3,9 +3,17 @@ from concourse.mybir import AluOpType, AxisListType, ActivationFunctionType
 
 E, CAP, S, NR = 2048, 256, 4, 8
 SRC_CHUNKS = [160, 320, 320, 320, 320, 320, 288]
-RELU_V = 704
-LAST_CHUNKS = [160, 256, 384, 480, 384, 256, 128]
+CALLS = ["f", "fn", "fn", "fn"]
+RELU_EARLY = 384
+RELU_V = {1: 704, 2: 704, 3: 896}
+LAST_CHUNKS = [224, 256, 352, 512, 352, 224, 128]
 NCH = len(LAST_CHUNKS)
+LAST_ORDER = {"v": "g0 z0 z1 r0 z2 z3 r3 z4 r4 z5 r5 z6 r6",
+              "a": "g1 g2 g3 r1 r2 g4 g5 g6 t0 t1 t2 t3 t4 t5 t6",
+              "t": "m0 m1 m2 m3 m4 m5 m6"}
+NL = (NR - 1) * NCH
+OUT_PARTS = [(0, 6), (6, 2)]
+OUT_BANKS = [(0, 1, 2, 3), (4, 5), (6,), (7,)]
 
 SCRATCH = {
     "mp1": ("sbuf", [128, 32], "int32"),
@@ -16,37 +24,38 @@ SCRATCH = {
     "offp": ("sbuf", [128, 32], "uint16"),
     "sndi": ("sbuf", [128, 128], "int32"),
     "srci": ("sbuf", [128, 256], "int32"),
+    "sndh": ("sbuf", [128, 128], "float16"),
+    "pmh": ("sbuf", [128, 128], "float16"),
     "tb": ("sbuf", [128, 388], "float32"),
-    "tp": ("sbuf", [128, 256], "float32"),
     "pm": ("sbuf", [128, 512], "float32"),
     "bias": ("sbuf", [128, 4], "float32"),
-    "pidx": ("sbuf", [128, 1], "int32"),
-    "bits": ("sbuf", [128, 4], "int32"),
-    "bitf": ("sbuf", [128, 8], "float32"),
-    "colh": ("sbuf", [128, 16], "float32"),
-    "offq": ("sbuf", [128, 16], "uint16"),
     "mi": ("sbuf", [128, 64], "int32"),
     "mj": ("sbuf", [128, 64], "int32"),
     "mask": ("sbuf", [128, 64], "float32"),
-    "bi": ("sbuf", [128, 128], "int32"),
-    "bj": ("sbuf", [128, 128], "int32"),
+    "one": ("sbuf", [128, NL], "float32"),
+    "ra": ("sbuf", [128, 128], "float32"),
+    "rt": ("sbuf", [128, 128], "float32"),
+    "bh": ("sbuf", [128, 128], "float32"),
     "bm": ("sbuf", [128, 128], "float32"),
     "bmq": ("sbuf", [128, 128], "float32"),
     "rep": ("sbuf", [128, 128], "float32"),
-    "aws": ("sbuf", [128, 16], "float32"),
-    "abs_": ("sbuf", [128, 1], "float32"),
-    "aqs": ("sbuf", [128, 1], "float32"),
-    "aql": ("sbuf", [128, NR - 1], "float32"),
-    "aqx": ("sbuf", [128, (NR - 1) * NCH], "float32"),
-    "awt": ("sbuf", [128, 128], "float32"),
+    "ex": ("sbuf", [128, NL], "float32"),
+    "abq": ("sbuf", [128, 8], "float32"),
+    "pad": ("sbuf", [128, 7], "float32"),
+    "aqd": ("dram", [128, 1], "float32"),
+    "aqe": ("dram", [NR - 1, 128, 1], "float32"),
+    "aqt": ("sbuf", [128, 128], "float32"),
+    "aql": ("sbuf", [128, NL], "float32"),
     "awb": ("sbuf", [128, 128], "float32"),
-    "abc": ("sbuf", [128, 2], "float32"),
+    "abc": ("sbuf", [128, 8], "float32"),
     "hh": ("sbuf", [128, E], "float32"),
     "th": ("sbuf", [128, E], "float32"),
     "acc": ("sbuf", [128, 8], "float32"),
-    "eo": ("sbuf", [128, 8], "float32"),
-    "land": ("sbuf", [128, (NR - 1) * NCH], "float32"),
-    "lq": ("sbuf", [128, (NR - 1) * NCH], "float32"),
+    "lm": ("sbuf", [128, 64], "float32"),
+    "wo": ("sbuf", [128, 1], "float32"),
+    "inv": ("sbuf", [128, 128], "float32"),
+    "land": ("sbuf", [128, NL], "float32"),
+    "lq": ("sbuf", [128, NL], "float32"),
     "sc": ("sbuf", [128, 4], "float32"),
     "wm": ("sbuf", [128, 64], "float32"),
     "yt": ("sbuf", [128, 256], "float32"),
@@ -61,7 +70,7 @@ for _s in range(S):
 for _b in range(8):
     SCRATCH["ps%d" % _b] = ("psum", [128, 512], "float32")
 
-SEMAPHORES = ["cv", "ca", "ct", "cg", "d_mp", "d_snd", "d_x", "d_src", "d_bs", "d_aw", "d_aq", "d_out",
+SEMAPHORES = ["cv", "ca", "ct", "cg", "d_mp", "d_snd", "d_x", "d_src", "d_bs", "d_aw", "d_ab", "d_aqd", "d_aqt", "d_out",
               "sent", "arr0", "arr1", "arr2", "arr3", "arrq", "arrs"]
 
 
@@ -72,14 +81,14 @@ def rounds_of(rank, cores, topo):
     i = same.index(rank)
     near = [same[(i + j) % len(same)] for j in range(1, len(same))]
     far = [other[(i + j) % len(other)] for j in range(len(other))]
+    left = {"f": far, "n": near}
     out = []
-    for j in range(max(len(near), len(far))):
-        if j < len(near) and j < len(far):
-            out.append([(far[j], topo.engines(me, cores[far[j]])[0::2]),
-                        (near[j], topo.engines(me, cores[near[j]])[1::2])])
-        else:
-            t = far[j] if j < len(far) else near[j]
-            out.append([(t, topo.engines(me, cores[t]))])
+    for kinds in CALLS:
+        call = []
+        for k, kind in enumerate(kinds):
+            t = left[kind].pop(0)
+            call.append((t, topo.engines(me, cores[t])[k::len(kinds)]))
+        out.append(call)
     return out
 
 
@@ -136,14 +145,11 @@ def rank_program(g, core, T, topo):
         rid, pid, _ = topo.addr(cores[r])
         return DstId(rid=rid, pnc=pid)
 
-    others = [t for t in range(NR) if t != rank]
+    others = [(rank + j) % NR for j in range(1, NR)]
     all_engs = topo.engines(core, cores[others[0]])
 
-    def to_all(deps, src, buf, n, sem):
-        dsts = []
-        for t in others:
-            j = [q for q in range(NR) if q != t].index(rank)
-            dsts.append(buf[:, n * j:n * j + n])
+    def to_all(deps, src, block, sem):
+        dsts = [block([q for q in range(NR) if q != t].index(rank)) for t in others]
         wait("g", *deps)
         g.remote_dma_fused([RemoteDMATransfer(dst_ids=[dst_id(t) for t in others], dma_engine_mask=bitmask(all_engs),
                                               remote_sem=T.sem[sem], srcs=[src], dsts=dsts)], local_sem=T.sem.sent)
@@ -154,49 +160,46 @@ def rank_program(g, core, T, topo):
     arrive = sum(len(engs) for q in range(NR) for call in rounds_of(q, cores, topo) for (t, engs) in call if t == rank)
     win = [T["win%d" % s] for s in range(S)]
     li = [T["li%d" % s] for s in range(S)]
+    zz = [T["zz%d" % s] for s in range(S)]
     ps = [T["ps%d" % b] for b in range(8)]
 
-    k_zero = v([], V.memset, T.aqs[:], 0.0)
+    k_zero = v([], V.memset, T.pad[0:16, :], 0.0)
+    v([], V.memset, T.one[0:16, :], 1.0)
+    k_one = v([], V.memset, T.inv[:], 1.0 / (NR * E))
+    dma("s", [], "d_aqd", T.aqd[0:16, :], T.aq[:])
     k_mp = dma("s", [], "d_mp", T.mp1[0:1, :], T.mp[:])
-    k_snd = dma("a", [], "d_snd", T.sndi[:], T.snd[:])
+    k_aqd = dma("a", [k_zero], "d_aqd", T.aqd[16:128, :], T.pad[0:16, :])
+    k_snd = dma("s", [], "d_snd", T.sndi[:], T.snd[:])
     for k in range(8):
-        k_x = dma("s" if k % 2 == 0 else "a", [], "d_x", win[0][16 * k:16 * k + 16, 0:E], T.x[:])
-        if k == 0:
-            k_aq = dma("s", [k_zero], "d_aq", T.aqs[0:16, :], T.aq[:])
-    k_src = dma("s", [], "d_src", T.srci[:], T.src[:])
-    k_bs = dma("a", [], "d_bs", T.tb[:, 384:385], T.bs[:])
-    dma("s", [], "d_aw", T.aws[0:16, :], T.aw[:])
-    k_aw = dma("s", [], "d_aw", T.abs_[0:16, :], T.ab[:])
+        k_x = dma("s" if k in (1, 3, 5) else "a", [], "d_x", win[0][16 * k:16 * k + 16, 0:E], T.x[:])
+    k_src = dma("s", [k_mp], "d_src", T.srci[:], T.src[:])
+    k_bs = dma("s", [], "d_bs", T.tb[:, 384:385], T.bs[:])
+    dma("s", [], "d_ab", T.abq[0:16, 0:1], T.ab[:])
+    k_ab = dma("s", [], "d_ab", T.abq[0:16, 4:5], T.aq[:])
 
-    k_cf = gp([], g.iota, T.cf[:], [[0, 8], [-1, 16]], 0, 1, allow_small_or_imprecise_dtypes=True)
+    fl = {"allow_small_or_imprecise_dtypes": True}
+    k_cf = gp([], g.iota, T.cf[:], [[0, 8], [-1, 16]], 0, 1, **fl)
     k_oi = gp([], g.iota, T.offi[:], [[1, 4], [4, 8]], 0, 0)
-    k_pi = gp([], g.iota, T.pidx[:], [[0, 1]], 0, 1)
-    k_ch = gp([], g.iota, T.colh[:], [[64, 2], [1, 8]], 0, 0, allow_small_or_imprecise_dtypes=True)
     k_mpb = gp([k_mp], g.partition_broadcast, T.mpb[:], T.mp1[0:1, :], 128)
-    k_aql = to_all([k_aq], T.aqs[:], T.aql, 1, "arrq")
+    k_aqe = to_all([k_aqd], T.aqd[:], lambda j: T.aqe[j], "arrq")
+    k_aqt = dma("s", [k_aqe], "d_aqt", T.aqt[0:NR - 1, :], T.aqe[:])
+    k = act([k_cf], T.ra[0:16, :], T.cf[0:16, :], F.Abs, scale=32.0)
+    k = act([k], T.rt[0:16, :], T.ra[0:16, :], F.Tanh, scale=-1.0, bias=16.0)
+    k_rep = act([k], T.rep[0:16, :], T.rt[0:16, :], F.Relu)
     k_cs = v([k_cf], V.tensor_scalar, T.cs[:], T.cf[:], 1.0 / 16, None, A.mult)
     k_op = v([k_oi], V.tensor_copy, T.offp[:], T.offi[:])
-    v([k_pi], V.tensor_scalar, T.bits[:, 0:1], T.pidx[:], 7, None, A.bitwise_and)
-    v([k_pi], V.tensor_scalar, T.bits[:, 1:2], T.pidx[:], 8, None, A.bitwise_and)
-    k = v([k_pi], V.tensor_scalar, T.bits[:, 2:3], T.pidx[:], 1, None, A.bitwise_and)
-    k = v([k], V.tensor_copy, T.bitf[:, 0:3], T.bits[:, 0:3])
-    k = v([k], V.tensor_scalar, T.bitf[:, 3:4], T.bitf[:, 0:1], 8.0, T.bitf[:, 1:2], A.mult, A.add)
-    k = v([k], V.tensor_scalar, T.bitf[:, 4:5], T.bitf[:, 2:3], -7.5, T.bitf[:, 3:4], A.mult, A.add)
-    k_oq = v([k, k_ch], V.tensor_scalar, T.offq[:], T.colh[:], T.bitf[:, 4:5], 2.0, A.add, A.mult)
-    k_sndf = v([k_snd], V.tensor_copy, T.tb[:, 256:384], T.sndi[:])
-
-    def perm(s):
-        return v([k_mpb, k_cs, k_op], V.tensor_tensor, T.pm[:, 128 * s:128 * s + 128],
-                 T.mpb[:, 0:32].indirect(T.offp[:, 8 * s:8 * s + 8]), T.cs[:], A.is_equal)
+    k_w0 = v([], V.memset, T.awb[:], 0.0)
+    k_sndh = v([k_snd], V.tensor_copy, T.sndh[:], T.sndi[:])
 
     def pmat(s):
         return T.pm[:, 128 * s:128 * s + 128]
 
-    k_p = perm(0)
-    k_m = mm([k_p, k_sndf], ps[0][:, 0:128], pmat(0), T.tb[:, 256:384])
-    k_p1 = perm(1)
+    def perm(s, out=None):
+        return v([k_mpb, k_cs, k_op], V.tensor_tensor, pmat(s) if out is None else out,
+                 T.mpb[:, 0:32].indirect(T.offp[:, 8 * s:8 * s + 8]), T.cs[:], A.is_equal)
+
+    k_m = mm([perm(0, T.pmh[:]), k_sndh], ps[0][:, 0:128], T.pmh[:], T.sndh[:])
     k_sl = v([k_m], V.tensor_copy, li[0][:, 256:384], ps[0][:, 0:128])
-    k_ms1 = mm([k_p1], ps[2][:, 0:128], pmat(1), T.tb[:, 256:384])
 
     def send(s, source, scale, deps):
         def gather(q, out, t, a=0, n=CAP):
@@ -228,11 +231,17 @@ def rank_program(g, core, T, topo):
             g.remote_dma_fused(trs, local_sem=T.sem.sent)
         return gather("a", win[s][:, lo:lo + CAP], rank)
 
-    def own_part(s, z, scale, deps):
-        h = RELU_V
-        a = v(deps, V.tensor_scalar, win[s][:, 0:h], z[:, 0:h], 0.0, scale, A.max, A.mult)
-        b = act(deps, win[s][:, h:E], z[:, h:E], F.Relu, scale=scale)
-        return [a, b]
+    def half(s):
+        return 0.25 if s == 1 else 0.5
+
+    def relu(q, s, lo, hi, deps):
+        if q == "v":
+            return v(deps, V.tensor_scalar, win[s][:, lo:hi], zz[s - 1][:, lo:hi], 0.0, half(s), A.max, A.mult)
+        return act(deps, win[s][:, lo:hi], zz[s - 1][:, lo:hi], F.Relu, scale=half(s))
+
+    def own_part(s, deps):
+        h = E - RELU_V[s]
+        return [relu("v", s, h, E, deps), relu("a", s, RELU_EARLY, h, deps)]
 
     def source(s, d, lo, n):
         c = 128 * d + lo // 16
@@ -245,104 +254,135 @@ def rank_program(g, core, T, topo):
         return act(deps, ga[:, lo:lo + n], source(s, 0, lo, n), F.Identity, bias=T.bias[:, s:s + 1])
 
     def second_source(s, lo, n, deps):
-        ga, zz = T["ga%d" % s], T["zz%d" % s]
-        return v(deps, V.tensor_tensor, zz[:, lo:lo + n], source(s, 1, lo, n), ga[:, lo:lo + n], A.add)
+        return v(deps, V.tensor_tensor, zz[s][:, lo:lo + n], source(s, 1, lo, n), T["ga%d" % s][:, lo:lo + n], A.add)
 
     def step(s, deps):
-        lo = 0
+        lo, early = 0, None
         for j, n in enumerate(SRC_CHUNKS):
             z = second_source(s, lo, n, [first_source("v" if j == 0 else "a", s, lo, n, deps)])
             lo += n
+            if early is None and lo >= RELU_EARLY:
+                early = z
+        relu("a", s + 1, 0, RELU_EARLY, [early])
         return z
 
-    def lists(s, k_mat):
-        v([k_mat], V.tensor_copy, li[s][:, 0:384], ps[s + 1][:, 0:384])
-        return v([k_mat], V.tensor_copy, T.bias[:, s:s + 1], ps[s + 1][:, 384:385])
+    def tables(s, bank, lo, hi, deps):
+        return mm(deps, ps[bank][:, lo:hi], pmat(s), T.tb[:, lo:hi])
+
+    def lists(s, bank, lo, hi, k_mat):
+        return v([k_mat], V.tensor_copy, li[s][:, lo:hi], ps[bank][:, lo:hi])
+
+    def bias(s, bank, k_mat):
+        return act([k_mat], T.bias[:, s:s + 1], ps[bank][:, 384:385], F.Identity, scale=2.0 if s == 0 else 1.0)
 
     k_own = send(0, win[0], None, [k_sl, k_x])
-    k_srcf = v([k_src], V.tensor_copy, T.tb[:, 0:256], T.srci[:])
-    mm([k_bs], ps[1][:, 256:257], pmat(0), T.tb[:, 384:385])
-    k_m0 = mm([k_srcf], ps[1][:, 0:256], pmat(0), T.tb[:, 0:256])
-    mm([], ps[5][:, 256:257], pmat(1), T.tb[:, 384:385])
-    k_m1 = mm([], ps[5][:, 0:256], pmat(1), T.tb[:, 0:256])
-    k_s1 = v([k_ms1], V.tensor_copy, li[1][:, 256:384], ps[2][:, 0:128])
-    k_m2 = mm([perm(2)], ps[3][:, 0:385], pmat(2), T.tb[:, 0:385])
-    v([k_m0], V.tensor_copy, li[0][:, 0:256], ps[1][:, 0:256])
-    k_l0 = v([k_m0], V.tensor_scalar, T.bias[:, 0:1], ps[1][:, 256:257], 2.0, None, A.mult)
+    mm([k_rep, k_ab], ps[6][:, 0:1], T.rep[0:16, :], T.abq[0:16, 0:1])
+    k = mm([], ps[6][:, 1:2], T.rep[0:16, :], T.abq[0:16, 4:5])
+    k_abc = act([k], T.abc[:, 0:2], ps[6][:, 0:2], F.Identity)
+    k = gp([k_one], g.affine_select, T.bh[:], T.inv[:], [[-16, 8], [0, 16]], A.is_ge, 0.0, 0, 1)
+    k_bm = gp([k], g.affine_select, T.bm[:], T.bh[:], [[16, 8], [0, 16]], A.is_ge, 0.0, 15, -1)
+    k_ex = gp([], g.affine_select, T.ex[0:16, :], T.one[0:16, 0:NL], [[-1, NR - 1], [0, NCH]], A.is_equal, 0.0, 0, 1)
     k_mi = gp([], g.iota, T.mi[:], [[1, 2], [-1, 32]], 32, 2)
-    k_bi = gp([], g.iota, T.bi[:], [[-16, 8], [0, 16]], 0, 1)
-    k_z = step(0, [("arr0", arrive), k_own, k_l0, k_x])
+    k_p0 = perm(0)
+    k_srcf = v([k_src], V.tensor_copy, T.tb[:, 0:256], T.srci[:])
+    k_b0 = bias(0, 2, tables(0, 2, 384, 385, [k_bs, k_p0]))
+    k_m0 = tables(0, 1, 0, 256, [k_srcf])
+    k_p1 = perm(1)
+    k_sndf = v([k_snd], V.tensor_copy, T.tb[:, 256:384], T.sndi[:])
+    k_ms1 = tables(1, 2, 256, 385, [k_p1, k_sndf, k_b0])
+    k_l0 = lists(0, 1, 0, 256, k_m0)
+    k_m1 = tables(1, 5, 0, 256, [])
+    k_s1 = lists(1, 2, 256, 384, k_ms1)
+    for k in range(8):
+        k_awb = dma("s", [k_w0, ("arr0", arrive)], "d_aw", T.awb[16 * k:16 * k + 16, 16 * k:16 * k + 16], T.aw[:])
+    k_z = step(0, [("arr0", arrive), k_own, k_l0, k_b0, k_x])
 
-    k_own = send(1, T.zz0, 0.25, [k_z, k_s1])
-    k_h = own_part(1, T.zz0, 0.25, [k_z])
-    v([k_m1], V.tensor_copy, li[1][:, 0:256], ps[5][:, 0:256])
-    k_l1 = v([k_m1], V.tensor_copy, T.bias[:, 1:2], ps[5][:, 256:257])
-    k_l2 = lists(2, k_m2)
-    k_rep = v([k_cf], V.tensor_scalar, T.rep[0:16, :], T.cf[0:16, :], 0.0, None, A.is_equal)
-    k_t1 = mm([k_rep, k_aw], ps[5][0:16, 0:128], T.aws[0:16, :], T.rep[0:16, :])
-    mm([], ps[7][:, 80:81], T.rep[0:16, :], T.abs_[0:16, :])
-    mm([k_aq], ps[7][:, 81:82], T.rep[0:16, :], T.aqs[0:16, :])
-    k_t3 = mm([k_aql], ps[7][:, 88:88 + NR - 1], T.rep[0:16, :], T.aql[0:16, :])
-    k_z = step(1, [("arr1", arrive), k_own, k_l1] + k_h)
+    k_own = send(1, zz[0], half(1), [k_z, k_s1])
+    k_m2 = tables(2, 3, 0, 385, [perm(2)])
+    k_l1 = lists(1, 5, 0, 256, k_m1)
+    k_h = own_part(1, [k_z])
+    k_b1 = bias(1, 2, k_s1)
+    k_s2 = lists(2, 3, 256, 384, k_m2)
+    k = mm([k_aqt, k_ex, k_abc], ps[6][0:16, 0:NL], T.aqt[0:NR - 1, 0:16], T.ex[0:NR - 1, :])
+    k = act([k], T.aql[0:16, :], ps[6][0:16, 0:NL], F.Identity)
+    k_aqx = mm([k], ps[7][:, 0:NL], T.rep[0:16, :], T.aql[0:16, :])
+    k_z = step(1, [("arr1", arrive), k_own, k_l1, k_b1] + k_h)
 
-    k_own = send(2, T.zz1, 0.5, [k_z, k_l2])
-    k_p3 = perm(3)
-    mm([k_p3], ps[4][:, 256:385], pmat(3), T.tb[:, 256:385])
-    k = v([k_oq, k_srcf], V.tensor_copy, T.tp[:], T.tb[:, 0:256].indirect(T.offq[:, 0:16]))
-    k_m3 = mm([k], ps[4][:, 0:256], pmat(3), T.tp[:])
-    k_h = own_part(2, T.zz1, 0.5, [k_z])
-    k_l3 = lists(3, k_m3)
-    k_z = step(2, [("arr2", arrive), k_own, k_l2] + k_h)
+    k_own = send(2, zz[1], half(2), [k_z, k_s2])
+    k_m3 = tables(3, 4, 256, 385, [perm(3)])
+    for d in range(2):
+        for first, n in OUT_PARTS:
+            for a in range(4):
+                for j in range(2):
+                    c = 128 * d + 16 * first
+                    k_m3s = mm([k_l1], ps[5][:, c + 2 * a + j:c + 16 * n:8], pmat(3),
+                               T.tb[:, c + 4 * n * a + j:c + 4 * n * a + 4 * n:2])
+    k_l2 = lists(2, 3, 0, 256, k_m2)
+    k_h = own_part(2, [k_z])
+    k_b2 = bias(2, 3, k_l2)
+    k_bmq = act([k_bm, k_abc], T.bmq[:], T.bm[:], F.Identity, scale=T.abc[:, 1:2])
+    k_s3 = lists(3, 4, 256, 384, k_m3)
+    k_z = step(2, [("arr2", arrive), k_own, k_l2, k_b2] + k_h)
 
-    k_own = send(3, T.zz2, 0.5, [k_z, k_l3])
-    k = v([k_t1], V.tensor_copy, T.awt[0:16, :], ps[5][0:16, 0:128])
-    k_t2 = mm([k], ps[6][:, 0:128], T.awt[0:16, :], T.rep[0:16, :])
-    k = v([k_bi], V.tensor_scalar, T.bj[:], T.bi[:], 4, None, A.arith_shift_right)
-    k_h = own_part(3, T.zz2, 0.5, [k_z])
-    k_bm = v([k], V.tensor_scalar, T.bm[:], T.bj[:], 0.0, None, A.is_equal)
-    k_abc = v([k_t3], V.tensor_copy, T.abc[:], ps[7][:, 80:82])
-    k_awb = v([k_t2, k_bm], V.tensor_tensor, T.awb[:], T.bm[:], ps[6][:, 0:128], A.mult)
-    k_bmq = v([k_abc], V.tensor_scalar, T.bmq[:], T.bm[:], T.abc[:, 1:2], None, A.mult)
-    deps = [("arr3", arrive), k_own, k_l3] + k_h
-    starts = [sum(LAST_CHUNKS[:j]) for j in range(NCH)]
-    gat = [first_source("v" if j == 0 else "a", 3, starts[j], LAST_CHUNKS[j], deps) for j in range(NCH)]
-    pre = []
-    for j in range(NCH):
-        lo, n = starts[j], LAST_CHUNKS[j]
-        kz = second_source(3, lo, n, [gat[j]])
-        kh = v([kz], V.tensor_scalar, T.hh[:, lo:lo + n], T.zz3[:, lo:lo + n], 0.0, None, A.max)
-        pre.append(mm([kh, k_awb], ps[j][:, 0:n], T.awb[:], T.hh[:, lo:lo + n]))
-    for j in range(NCH):
-        lo, n = starts[j], LAST_CHUNKS[j]
-        k_t = act([pre[j], k_abc], T.th[:, lo:lo + n], ps[j][:, 0:n], F.Tanh, bias=T.abc[:, 0:1],
-                  accum_out=T.acc[:, j:j + 1])
-
-    k_land = to_all([k_t], T.acc[:, 0:NCH], T.land, NCH, "arrs")
-    inv = 1.0 / (NR * E)
-    nl = (NR - 1) * NCH
-    for j in range(NR - 1):
-        k_aqx = v([k_t3], V.tensor_scalar, T.aqx[:, NCH * j:NCH * j + NCH], T.cf[:, 0:NCH], 0.0,
-                  ps[7][:, 88 + j:89 + j], A.mult, A.add)
+    k_own = send(3, zz[2], half(3), [k_z, k_s3])
+    k_l3 = lists(3, 5, 0, 256, k_m3s)
+    k_h = own_part(3, [k_z])
+    k_b3 = bias(3, 4, k_s3)
     k = v([k_mi], V.tensor_scalar, T.mj[:], T.mi[:], 31, None, A.bitwise_and)
-    k_mask = v([k], V.tensor_scalar, T.mask[:], T.mj[:], 0.0, None, A.is_equal)
-    k = mm([k_t, k_bmq], ps[3][:, 0:NCH], T.bmq[:], T.acc[:, 0:NCH])
-    k_eo = act([k], T.eo[:, 0:NCH], ps[3][:, 0:NCH], F.Exp, scale=inv)
-    k = v([k_land, k_aqx], V.tensor_tensor, T.lq[:], T.land[:], T.aqx[:], A.mult)
-    k = mm([k], ps[4][:, 0:nl], T.bm[:], T.lq[:])
-    k = v([k], V.tensor_reduce, T.sc[:, 2:3], ps[4][:, 0:nl], X, A.add)
-    k_er = act([k], T.sc[:, 3:4], T.sc[:, 2:3], F.Exp, scale=inv)
-    k_eo = v([k_eo], V.tensor_reduce, T.sc[:, 1:2], T.eo[:, 0:NCH], X, A.mult)
-    k_wm = v([k_er, k_eo, k_mask], V.tensor_scalar, T.wm[:], T.mask[:], T.sc[:, 1:2], T.sc[:, 3:4], A.mult, A.mult)
-    dma("s", [k_wm], "d_out", T.w[:], T.wm[0:128:16, 0:1])
+    k_mask = v([k], V.tensor_scalar, T.mask[:], T.mj[:], 0.0, -200.0, A.not_equal, A.mult)
+    deps = [("arr3", arrive), k_own, k_l3, k_b3] + k_h
+    starts = [sum(LAST_CHUNKS[:j]) for j in range(NCH)]
 
-    for bank, bs_ in enumerate([(0, 1, 2, 3), (4, 5, 6), (7,)]):
+    def last(op, q, j, tok):
+        lo, n = starts[j], LAST_CHUNKS[j]
+        hh = T.hh[:, lo:lo + n]
+        if op == "g":
+            return first_source(q, 3, lo, n, deps)
+        if op == "z":
+            return second_source(3, lo, n, [tok] + deps)
+        if op == "r" and q == "v":
+            return v([tok], V.tensor_scalar, hh, zz[3][:, lo:lo + n], 0.0, None, A.max)
+        if op == "r":
+            return act([tok], hh, zz[3][:, lo:lo + n], F.Relu)
+        if op == "m":
+            return mm([tok, k_awb], ps[j][:, 0:n], T.awb[:], hh)
+        return act([tok, k_abc], T.th[:, lo:lo + n], ps[j][:, 0:n], F.Tanh, bias=T.abc[:, 0:1], accum_out=T.acc[:, j:j + 1])
+
+    before = {"g": None, "z": "g", "r": "z", "m": "r", "t": "m"}
+    todo = {q: order.split() for q, order in LAST_ORDER.items()}
+    made = {}
+    while any(todo.values()):
+        for q, ops in todo.items():
+            while ops and (before[ops[0][0]] is None or (before[ops[0][0]], ops[0][1]) in made):
+                op, j = ops.pop(0)
+                made[(op, j)] = last(op, q, int(j), made.get((before[op], j)))
+    k_t = ("ca", count["ca"])
+
+    k_land = to_all([k_t], T.acc[:, 0:NCH], lambda j: T.land[:, NCH * j:NCH * j + NCH], "arrs")
+    k = mm([k_t, k_bmq], ps[3][:, 0:NCH], T.bmq[:], T.acc[:, 0:NCH])
+    k_so = v([k], V.tensor_reduce, T.sc[:, 0:1], ps[3][:, 0:NCH], X, A.add)
+    k_eo = act([k_so], T.sc[:, 1:2], T.sc[:, 0:1], F.Exp)
+    k_lm = v([k_so, k_mask], V.tensor_scalar, T.lm[:], T.mask[:], T.sc[:, 0:1], None, A.add)
+    k = v([k_land, k_aqx], V.tensor_tensor, T.lq[:], T.land[:], ps[7][:, 0:NL], A.mult)
+    k = mm([k, k_bm], ps[4][:, 0:NL], T.bm[:], T.lq[:])
+    k = v([k], V.tensor_reduce, T.sc[:, 2:3], ps[4][:, 0:NL], X, A.add)
+    k_wm = act([k, k_lm], T.wm[:], T.lm[:], F.Exp, bias=T.sc[:, 2:3])
+    k = act([], T.sc[:, 3:4], T.sc[:, 2:3], F.Exp)
+    k = act([k, k_eo], T.wo[:], T.sc[:, 3:4], F.Identity, scale=T.sc[:, 1:2])
+    dma("s", [k], "d_out", T.w[:], T.wo[0:128:16, 0:1])
+
+    for bank, bs_ in enumerate(OUT_BANKS):
+        first, n = [p for p in OUT_PARTS if p[0] <= bs_[0] < p[0] + p[1]][0]
         for i, b in enumerate(bs_):
             for par in range(2):
-                c = 128 * (2 * b + par)
+                c = 128 * (2 * first + n * par + b - first)
                 k = mm([k_wm], ps[bank][:, 32 * i:32 * i + 32], T.hh[:, c:c + 128], T.wm[:, 32 * par:32 * par + 32],
                        par == 0, par == 1)
         k_y = v([k], V.transpose, T.yt[:, 32 * bs_[0]:32 * bs_[-1] + 32], ps[bank][:, 0:32 * len(bs_)])
-    for a in range(4):
-        k_o = dma("s" if a % 2 == 0 else "a", [k_y], "d_out", T.y[:, 512 * a:512 * a + 512], T.yt[32 * a:32 * a + 32, :])
+        if bs_[-1] == first + n - 1:
+            for a in range(4):
+                c = 256 * first + 64 * n * a
+                k_o = dma("s" if a % 2 == 0 else "a", [k_y], "d_out", T.y[:, c:c + 64 * n],
+                          T.yt[32 * a:32 * a + 32, 32 * first:32 * (first + n)])
     wait("s", k_o)
     wait("g", *[(n, count[n]) for n in ("sent", "cg", "ct", "ca", "cv")])

from concourse.bass import DstId, RemoteDMATransfer
from concourse.mybir import AluOpType, AxisListType, ActivationFunctionType

E, CAP, S, NR = 2048, 256, 4, 8
SRC_CHUNKS = [160, 320, 320, 320, 320, 320, 288]
CALLS = ["f", "fn", "fn", "fn"]
RELU_EARLY = 384
RELU_V = {1: 704, 2: 704, 3: 896}
LAST_CHUNKS = [224, 256, 352, 512, 352, 224, 128]
NCH = len(LAST_CHUNKS)
LAST_ORDER = {"v": "g0 z0 z1 r0 z2 z3 r3 z4 r4 z5 r5 z6 r6",
              "a": "g1 g2 g3 r1 r2 g4 g5 g6 t0 t1 t2 t3 t4 t5 t6",
              "t": "m0 m1 m2 m3 m4 m5 m6"}
NL = (NR - 1) * NCH
OUT_PARTS = [(0, 6), (6, 2)]
OUT_BANKS = [(0, 1, 2, 3), (4, 5), (6,), (7,)]

SCRATCH = {
    "mp1": ("sbuf", [128, 32], "int32"),
    "mpb": ("sbuf", [128, 32], "int32"),
    "cf": ("sbuf", [128, 128], "float32"),
    "cs": ("sbuf", [128, 128], "float32"),
    "offi": ("sbuf", [128, 32], "int32"),
    "offp": ("sbuf", [128, 32], "uint16"),
    "sndi": ("sbuf", [128, 128], "int32"),
    "srci": ("sbuf", [128, 256], "int32"),
    "sndh": ("sbuf", [128, 128], "float16"),
    "pmh": ("sbuf", [128, 128], "float16"),
    "tb": ("sbuf", [128, 388], "float32"),
    "pm": ("sbuf", [128, 512], "float32"),
    "bias": ("sbuf", [128, 4], "float32"),
    "mi": ("sbuf", [128, 64], "int32"),
    "mj": ("sbuf", [128, 64], "int32"),
    "mask": ("sbuf", [128, 64], "float32"),
    "one": ("sbuf", [128, NL], "float32"),
    "ra": ("sbuf", [128, 128], "float32"),
    "rt": ("sbuf", [128, 128], "float32"),
    "bh": ("sbuf", [128, 128], "float32"),
    "bm": ("sbuf", [128, 128], "float32"),
    "bmq": ("sbuf", [128, 128], "float32"),
    "rep": ("sbuf", [128, 128], "float32"),
    "ex": ("sbuf", [128, NL], "float32"),
    "abq": ("sbuf", [128, 8], "float32"),
    "pad": ("sbuf", [128, 7], "float32"),
    "aqd": ("dram", [128, 1], "float32"),
    "aqe": ("dram", [NR - 1, 128, 1], "float32"),
    "aqt": ("sbuf", [128, 128], "float32"),
    "aql": ("sbuf", [128, NL], "float32"),
    "awb": ("sbuf", [128, 128], "float32"),
    "abc": ("sbuf", [128, 8], "float32"),
    "hh": ("sbuf", [128, E], "float32"),
    "th": ("sbuf", [128, E], "float32"),
    "acc": ("sbuf", [128, 8], "float32"),
    "lm": ("sbuf", [128, 64], "float32"),
    "wo": ("sbuf", [128, 1], "float32"),
    "inv": ("sbuf", [128, 128], "float32"),
    "land": ("sbuf", [128, NL], "float32"),
    "lq": ("sbuf", [128, NL], "float32"),
    "sc": ("sbuf", [128, 4], "float32"),
    "wm": ("sbuf", [128, 64], "float32"),
    "yt": ("sbuf", [128, 256], "float32"),
}
for _s in range(S):
    _d = "bfloat16" if _s == 0 else "float32"
    SCRATCH["li%d" % _s] = ("sbuf", [128, 384], "uint16")
    SCRATCH["win%d" % _s] = ("sbuf", [128, 2 * E], _d)
    SCRATCH["sb%d" % _s] = ("sbuf", [128, (NR - 1) * CAP], _d)
    SCRATCH["ga%d" % _s] = ("sbuf", [128, E], "float32")
    SCRATCH["zz%d" % _s] = ("sbuf", [128, E], "float32")
for _b in range(8):
    SCRATCH["ps%d" % _b] = ("psum", [128, 512], "float32")

SEMAPHORES = ["cv", "ca", "ct", "cg", "d_mp", "d_snd", "d_x", "d_src", "d_bs", "d_aw", "d_ab", "d_aqd", "d_aqt", "d_out",
              "sent", "arr0", "arr1", "arr2", "arr3", "arrq", "arrs"]


def rounds_of(rank, cores, topo):
    me = cores[rank]
    same = [r for r in range(len(cores)) if topo.die(cores[r]) == topo.die(me)]
    other = [r for r in range(len(cores)) if topo.die(cores[r]) != topo.die(me)]
    i = same.index(rank)
    near = [same[(i + j) % len(same)] for j in range(1, len(same))]
    far = [other[(i + j) % len(other)] for j in range(len(other))]
    left = {"f": far, "n": near}
    out = []
    for kinds in CALLS:
        call = []
        for k, kind in enumerate(kinds):
            t = left[kind].pop(0)
            call.append((t, topo.engines(me, cores[t])[k::len(kinds)]))
        out.append(call)
    return out


def rank_program(g, core, T, topo):
    rank = T.rank_of(core)
    if rank is None:
        return
    cores = list(T.cores)
    A, F, X = AluOpType, ActivationFunctionType, AxisListType.X
    V, ACT, PE, SY = g.vector, g.scalar, g.tensor, g.sync
    queues = {"v": V, "a": ACT, "t": PE, "g": g, "s": SY}
    count = {"sent": 0}
    seen = {}

    def wait(q, *toks):
        need = {}
        for tok in toks:
            if tok is not None:
                need[tok[0]] = max(need.get(tok[0], 0), tok[1])
        for name, val in need.items():
            if seen.get((q, name), 0) < val:
                queues[q].wait_ge(T.sem[name], val)
                seen[(q, name)] = val

    def done(ins, name, n=1):
        ins.then_inc(T.sem[name], n)
        count[name] = count.get(name, 0) + n
        return (name, count[name])

    def v(deps, fn, *a, **k):
        wait("v", *deps)
        return done(fn(*a, **k), "cv")

    def act(deps, *a, **k):
        wait("a", *deps)
        return done(ACT.activation(*a, **k), "ca")

    def mm(deps, out, lhsT, rhs, start=True, stop=True):
        wait("t", *deps)
        return done(PE.matmul(out, lhsT, rhs, start, stop), "ct")

    def gp(deps, fn, *a, **k):
        wait("g", *deps)
        return done(fn(*a, **k), "cg")

    def dma(q, deps, sem, out, in_):
        wait(q, *deps)
        return done(queues[q].dma_start(out, in_), sem, 16)

    def bitmask(engs):
        return sum(1 << e for e in engs)

    def dst_id(r):
        rid, pid, _ = topo.addr(cores[r])
        return DstId(rid=rid, pnc=pid)

    others = [(rank + j) % NR for j in range(1, NR)]
    all_engs = topo.engines(core, cores[others[0]])

    def to_all(deps, src, block, sem):
        dsts = [block([q for q in range(NR) if q != t].index(rank)) for t in others]
        wait("g", *deps)
        g.remote_dma_fused([RemoteDMATransfer(dst_ids=[dst_id(t) for t in others], dma_engine_mask=bitmask(all_engs),
                                              remote_sem=T.sem[sem], srcs=[src], dsts=dsts)], local_sem=T.sem.sent)
        count["sent"] += len(all_engs)
        return (sem, (NR - 1) * len(all_engs))

    rounds = rounds_of(rank, cores, topo)
    arrive = sum(len(engs) for q in range(NR) for call in rounds_of(q, cores, topo) for (t, engs) in call if t == rank)
    win = [T["win%d" % s] for s in range(S)]
    li = [T["li%d" % s] for s in range(S)]
    zz = [T["zz%d" % s] for s in range(S)]
    ps = [T["ps%d" % b] for b in range(8)]

    k_zero = v([], V.memset, T.pad[0:16, :], 0.0)
    v([], V.memset, T.one[0:16, :], 1.0)
    k_one = v([], V.memset, T.inv[:], 1.0 / (NR * E))
    dma("s", [], "d_aqd", T.aqd[0:16, :], T.aq[:])
    k_mp = dma("s", [], "d_mp", T.mp1[0:1, :], T.mp[:])
    k_aqd = dma("a", [k_zero], "d_aqd", T.aqd[16:128, :], T.pad[0:16, :])
    k_snd = dma("s", [], "d_snd", T.sndi[:], T.snd[:])
    for k in range(8):
        k_x = dma("s" if k in (1, 3, 5) else "a", [], "d_x", win[0][16 * k:16 * k + 16, 0:E], T.x[:])
    k_src = dma("s", [k_mp], "d_src", T.srci[:], T.src[:])
    k_bs = dma("s", [], "d_bs", T.tb[:, 384:385], T.bs[:])
    dma("s", [], "d_ab", T.abq[0:16, 0:1], T.ab[:])
    k_ab = dma("s", [], "d_ab", T.abq[0:16, 4:5], T.aq[:])

    fl = {"allow_small_or_imprecise_dtypes": True}
    k_cf = gp([], g.iota, T.cf[:], [[0, 8], [-1, 16]], 0, 1, **fl)
    k_oi = gp([], g.iota, T.offi[:], [[1, 4], [4, 8]], 0, 0)
    k_mpb = gp([k_mp], g.partition_broadcast, T.mpb[:], T.mp1[0:1, :], 128)
    k_aqe = to_all([k_aqd], T.aqd[:], lambda j: T.aqe[j], "arrq")
    k_aqt = dma("s", [k_aqe], "d_aqt", T.aqt[0:NR - 1, :], T.aqe[:])
    k = act([k_cf], T.ra[0:16, :], T.cf[0:16, :], F.Abs, scale=32.0)
    k = act([k], T.rt[0:16, :], T.ra[0:16, :], F.Tanh, scale=-1.0, bias=16.0)
    k_rep = act([k], T.rep[0:16, :], T.rt[0:16, :], F.Relu)
    k_cs = v([k_cf], V.tensor_scalar, T.cs[:], T.cf[:], 1.0 / 16, None, A.mult)
    k_op = v([k_oi], V.tensor_copy, T.offp[:], T.offi[:])
    k_w0 = v([], V.memset, T.awb[:], 0.0)
    k_sndh = v([k_snd], V.tensor_copy, T.sndh[:], T.sndi[:])

    def pmat(s):
        return T.pm[:, 128 * s:128 * s + 128]

    def perm(s, out=None):
        return v([k_mpb, k_cs, k_op], V.tensor_tensor, pmat(s) if out is None else out,
                 T.mpb[:, 0:32].indirect(T.offp[:, 8 * s:8 * s + 8]), T.cs[:], A.is_equal)

    k_m = mm([perm(0, T.pmh[:]), k_sndh], ps[0][:, 0:128], T.pmh[:], T.sndh[:])
    k_sl = v([k_m], V.tensor_copy, li[0][:, 256:384], ps[0][:, 0:128])

    def send(s, source, scale, deps):
        def gather(q, out, t, a=0, n=CAP):
            c = 256 + 16 * t + a // 16
            src_ap = source[:, 0:E].indirect(li[s][:, c:c + n // 16])
            if q == "v":
                if scale is None:
                    return v(deps, V.tensor_copy, out, src_ap)
                return v(deps, V.tensor_scalar, out, src_ap, 0.0, scale, A.max, A.mult)
            if scale is None:
                return act(deps, out, src_ap, F.Identity)
            return act(deps, out, src_ap, F.Relu, scale=scale)
        pos = 0
        lo = E + CAP * rank
        sb = T["sb%d" % s]
        for call in rounds:
            toks, trs = [], []
            for q, (t, engs) in zip(("v", "a"), call):
                if len(call) == 1:
                    h = CAP // 2
                    toks += [gather("v", sb[:, pos:pos + h], t, 0, h), gather("a", sb[:, pos + h:pos + CAP], t, h, h)]
                else:
                    toks.append(gather(q, sb[:, pos:pos + CAP], t))
                trs.append(RemoteDMATransfer(dst_ids=[dst_id(t)], dma_engine_mask=bitmask(engs), remote_sem=T.sem["arr%d" % s],
                                             src=sb[:, pos:pos + CAP], dst=win[s][:, lo:lo + CAP]))
                pos += CAP
                count["sent"] += len(engs)
            wait("g", *toks)
            g.remote_dma_fused(trs, local_sem=T.sem.sent)
        return gather("a", win[s][:, lo:lo + CAP], rank)

    def half(s):
        return 0.25 if s == 1 else 0.5

    def relu(q, s, lo, hi, deps):
        if q == "v":
            return v(deps, V.tensor_scalar, win[s][:, lo:hi], zz[s - 1][:, lo:hi], 0.0, half(s), A.max, A.mult)
        return act(deps, win[s][:, lo:hi], zz[s - 1][:, lo:hi], F.Relu, scale=half(s))

    def own_part(s, deps):
        h = E - RELU_V[s]
        return [relu("v", s, h, E, deps), relu("a", s, RELU_EARLY, h, deps)]

    def source(s, d, lo, n):
        c = 128 * d + lo // 16
        return win[s][:, :].indirect(li[s][:, c:c + n // 16])

    def first_source(q, s, lo, n, deps):
        ga = T["ga%d" % s]
        if q == "v":
            return v(deps, V.tensor_scalar, ga[:, lo:lo + n], source(s, 0, lo, n), T.bias[:, s:s + 1], None, A.add)
        return act(deps, ga[:, lo:lo + n], source(s, 0, lo, n), F.Identity, bias=T.bias[:, s:s + 1])

    def second_source(s, lo, n, deps):
        return v(deps, V.tensor_tensor, zz[s][:, lo:lo + n], source(s, 1, lo, n), T["ga%d" % s][:, lo:lo + n], A.add)

    def step(s, deps):
        lo, early = 0, None
        for j, n in enumerate(SRC_CHUNKS):
            z = second_source(s, lo, n, [first_source("v" if j == 0 else "a", s, lo, n, deps)])
            lo += n
            if early is None and lo >= RELU_EARLY:
                early = z
        relu("a", s + 1, 0, RELU_EARLY, [early])
        return z

    def tables(s, bank, lo, hi, deps):
        return mm(deps, ps[bank][:, lo:hi], pmat(s), T.tb[:, lo:hi])

    def lists(s, bank, lo, hi, k_mat):
        return v([k_mat], V.tensor_copy, li[s][:, lo:hi], ps[bank][:, lo:hi])

    def bias(s, bank, k_mat):
        return act([k_mat], T.bias[:, s:s + 1], ps[bank][:, 384:385], F.Identity, scale=2.0 if s == 0 else 1.0)

    k_own = send(0, win[0], None, [k_sl, k_x])
    mm([k_rep, k_ab], ps[6][:, 0:1], T.rep[0:16, :], T.abq[0:16, 0:1])
    k = mm([], ps[6][:, 1:2], T.rep[0:16, :], T.abq[0:16, 4:5])
    k_abc = act([k], T.abc[:, 0:2], ps[6][:, 0:2], F.Identity)
    k = gp([k_one], g.affine_select, T.bh[:], T.inv[:], [[-16, 8], [0, 16]], A.is_ge, 0.0, 0, 1)
    k_bm = gp([k], g.affine_select, T.bm[:], T.bh[:], [[16, 8], [0, 16]], A.is_ge, 0.0, 15, -1)
    k_ex = gp([], g.affine_select, T.ex[0:16, :], T.one[0:16, 0:NL], [[-1, NR - 1], [0, NCH]], A.is_equal, 0.0, 0, 1)
    k_mi = gp([], g.iota, T.mi[:], [[1, 2], [-1, 32]], 32, 2)
    k_p0 = perm(0)
    k_srcf = v([k_src], V.tensor_copy, T.tb[:, 0:256], T.srci[:])
    k_b0 = bias(0, 2, tables(0, 2, 384, 385, [k_bs, k_p0]))
    k_m0 = tables(0, 1, 0, 256, [k_srcf])
    k_p1 = perm(1)
    k_sndf = v([k_snd], V.tensor_copy, T.tb[:, 256:384], T.sndi[:])
    k_ms1 = tables(1, 2, 256, 385, [k_p1, k_sndf, k_b0])
    k_l0 = lists(0, 1, 0, 256, k_m0)
    k_m1 = tables(1, 5, 0, 256, [])
    k_s1 = lists(1, 2, 256, 384, k_ms1)
    for k in range(8):
        k_awb = dma("s", [k_w0, ("arr0", arrive)], "d_aw", T.awb[16 * k:16 * k + 16, 16 * k:16 * k + 16], T.aw[:])
    k_z = step(0, [("arr0", arrive), k_own, k_l0, k_b0, k_x])

    k_own = send(1, zz[0], half(1), [k_z, k_s1])
    k_m2 = tables(2, 3, 0, 385, [perm(2)])
    k_l1 = lists(1, 5, 0, 256, k_m1)
    k_h = own_part(1, [k_z])
    k_b1 = bias(1, 2, k_s1)
    k_s2 = lists(2, 3, 256, 384, k_m2)
    k = mm([k_aqt, k_ex, k_abc], ps[6][0:16, 0:NL], T.aqt[0:NR - 1, 0:16], T.ex[0:NR - 1, :])
    k = act([k], T.aql[0:16, :], ps[6][0:16, 0:NL], F.Identity)
    k_aqx = mm([k], ps[7][:, 0:NL], T.rep[0:16, :], T.aql[0:16, :])
    k_z = step(1, [("arr1", arrive), k_own, k_l1, k_b1] + k_h)

    k_own = send(2, zz[1], half(2), [k_z, k_s2])
    k_m3 = tables(3, 4, 256, 385, [perm(3)])
    for d in range(2):
        for first, n in OUT_PARTS:
            for a in range(4):
                for j in range(2):
                    c = 128 * d + 16 * first
                    k_m3s = mm([k_l1], ps[5][:, c + 2 * a + j:c + 16 * n:8], pmat(3),
                               T.tb[:, c + 4 * n * a + j:c + 4 * n * a + 4 * n:2])
    k_l2 = lists(2, 3, 0, 256, k_m2)
    k_h = own_part(2, [k_z])
    k_b2 = bias(2, 3, k_l2)
    k_bmq = act([k_bm, k_abc], T.bmq[:], T.bm[:], F.Identity, scale=T.abc[:, 1:2])
    k_s3 = lists(3, 4, 256, 384, k_m3)
    k_z = step(2, [("arr2", arrive), k_own, k_l2, k_b2] + k_h)

    k_own = send(3, zz[2], half(3), [k_z, k_s3])
    k_l3 = lists(3, 5, 0, 256, k_m3s)
    k_h = own_part(3, [k_z])
    k_b3 = bias(3, 4, k_s3)
    k = v([k_mi], V.tensor_scalar, T.mj[:], T.mi[:], 31, None, A.bitwise_and)
    k_mask = v([k], V.tensor_scalar, T.mask[:], T.mj[:], 0.0, -200.0, A.not_equal, A.mult)
    deps = [("arr3", arrive), k_own, k_l3, k_b3] + k_h
    starts = [sum(LAST_CHUNKS[:j]) for j in range(NCH)]

    def last(op, q, j, tok):
        lo, n = starts[j], LAST_CHUNKS[j]
        hh = T.hh[:, lo:lo + n]
        if op == "g":
            return first_source(q, 3, lo, n, deps)
        if op == "z":
            return second_source(3, lo, n, [tok] + deps)
        if op == "r" and q == "v":
            return v([tok], V.tensor_scalar, hh, zz[3][:, lo:lo + n], 0.0, None, A.max)
        if op == "r":
            return act([tok], hh, zz[3][:, lo:lo + n], F.Relu)
        if op == "m":
            return mm([tok, k_awb], ps[j][:, 0:n], T.awb[:], hh)
        return act([tok, k_abc], T.th[:, lo:lo + n], ps[j][:, 0:n], F.Tanh, bias=T.abc[:, 0:1], accum_out=T.acc[:, j:j + 1])

    before = {"g": None, "z": "g", "r": "z", "m": "r", "t": "m"}
    todo = {q: order.split() for q, order in LAST_ORDER.items()}
    made = {}
    while any(todo.values()):
        for q, ops in todo.items():
            while ops and (before[ops[0][0]] is None or (before[ops[0][0]], ops[0][1]) in made):
                op, j = ops.pop(0)
                made[(op, j)] = last(op, q, int(j), made.get((before[op], j)))
    k_t = ("ca", count["ca"])

    k_land = to_all([k_t], T.acc[:, 0:NCH], lambda j: T.land[:, NCH * j:NCH * j + NCH], "arrs")
    k = mm([k_t, k_bmq], ps[3][:, 0:NCH], T.bmq[:], T.acc[:, 0:NCH])
    k_so = v([k], V.tensor_reduce, T.sc[:, 0:1], ps[3][:, 0:NCH], X, A.add)
    k_eo = act([k_so], T.sc[:, 1:2], T.sc[:, 0:1], F.Exp)
    k_lm = v([k_so, k_mask], V.tensor_scalar, T.lm[:], T.mask[:], T.sc[:, 0:1], None, A.add)
    k = v([k_land, k_aqx], V.tensor_tensor, T.lq[:], T.land[:], ps[7][:, 0:NL], A.mult)
    k = mm([k, k_bm], ps[4][:, 0:NL], T.bm[:], T.lq[:])
    k = v([k], V.tensor_reduce, T.sc[:, 2:3], ps[4][:, 0:NL], X, A.add)
    k_wm = act([k, k_lm], T.wm[:], T.lm[:], F.Exp, bias=T.sc[:, 2:3])
    k = act([], T.sc[:, 3:4], T.sc[:, 2:3], F.Exp)
    k = act([k, k_eo], T.wo[:], T.sc[:, 3:4], F.Identity, scale=T.sc[:, 1:2])
    dma("s", [k], "d_out", T.w[:], T.wo[0:128:16, 0:1])

    for bank, bs_ in enumerate(OUT_BANKS):
        first, n = [p for p in OUT_PARTS if p[0] <= bs_[0] < p[0] + p[1]][0]
        for i, b in enumerate(bs_):
            for par in range(2):
                c = 128 * (2 * first + n * par + b - first)
                k = mm([k_wm], ps[bank][:, 32 * i:32 * i + 32], T.hh[:, c:c + 128], T.wm[:, 32 * par:32 * par + 32],
                       par == 0, par == 1)
        k_y = v([k], V.transpose, T.yt[:, 32 * bs_[0]:32 * bs_[-1] + 32], ps[bank][:, 0:32 * len(bs_)])
        if bs_[-1] == first + n - 1:
            for a in range(4):
                c = 256 * first + 64 * n * a
                k_o = dma("s" if a % 2 == 0 else "a", [k_y], "d_out", T.y[:, c:c + 64 * n],
                          T.yt[32 * a:32 * a + 32, 32 * first:32 * (first + n)])
    wait("s", k_o)
    wait("g", *[(n, count[n]) for n in ("sent", "cg", "ct", "ca", "cv")])
